import numpy as np
import ml_dtypes


def mxq(x, axis, fmt="e4m3"):
    dtype, down = {"e4m3": (ml_dtypes.float8_e4m3fn, 7), "e5m2": (ml_dtypes.float8_e5m2, 14)}[fmt]
    v = np.moveaxis(np.asarray(x, np.float32).astype(ml_dtypes.bfloat16).astype(np.float64), axis, -1)
    blocks = v.reshape(v.shape[:-1] + (-1, 32))
    amax = np.abs(blocks).max(-1, keepdims=True)
    byte = np.maximum(np.where(amax > 0, np.frexp(amax)[1] - 1 + 127, 0) - down, 1)
    scale = np.exp2(byte - 127.0)
    codes = (blocks / scale).astype(np.float32).astype(dtype).astype(np.float64)
    return np.moveaxis((codes * scale).reshape(v.shape), -1, axis)


WIDE = False


def mx_kscale(k):
    if not WIDE:
        return np.ones(k)
    levels = np.array([10, -10, 5, -5, 0])
    if k % 512:
        return np.exp2(np.random.permutation(np.resize(levels, k // 32))).repeat(32)
    a = np.empty((k // 512, 16))
    for p in range(k // 512):
        a[p, :8] = np.random.permutation(np.resize(levels, 8))
        for g in range(8):
            far = levels[np.abs(levels - a[p, g]) >= 10]
            a[p, g + 8] = far[np.random.randint(len(far))]
    return np.exp2(a.ravel()).repeat(32)


def f64(x):
    return np.asarray(x).astype(np.float64)


def striped(idx):
    return np.tile(idx.reshape(-1, 16).T, (8, 1)).astype(np.uint16)


def unstriped(offs):
    return offs[:16].T.reshape(-1).astype(np.int64)


def pack_weight(w):
    k, n = w.shape
    w = f64(np.asarray(w, np.float32).astype(ml_dtypes.bfloat16)).reshape(k // 32, 32, n)
    amax = np.abs(w).max(1)
    byte = np.clip(np.where(amax > 0, np.frexp(amax)[1] - 1 + 127 - 7, 1), 1, 254)
    scaled = (w * np.exp2(127.0 - byte)[:, None, :]).reshape(k, n).astype(np.float32)
    words = np.ascontiguousarray(scaled.reshape(k // 512, 128, 4, n).transpose(0, 1, 3, 2)).astype(ml_dtypes.float8_e4m3fn).view(np.uint8)
    return words, np.ascontiguousarray(byte.astype(np.uint8).reshape(k // 512, 16, n))


def unpack_weight(words, scales):
    g, p, n, _ = words.shape
    vals = np.ascontiguousarray(words).view(ml_dtypes.float8_e4m3fn).astype(np.float64) * np.repeat(np.exp2(scales.astype(np.float64) - 127.0), 8, axis=1)[..., None]
    return vals.transpose(0, 1, 3, 2).reshape(g * 512, n)


K, T, S, D, H, N = 512, 2048, 1024, 2, 512, 256


def setup_inputs():
    n = np.random.standard_normal
    s = mx_kscale(K)[:, None]
    u = mx_kscale(H)
    packed_xT = pack_weight(n((K, T)) * s)
    return {
        "x_words": packed_xT[0],
        "x_scales": packed_xT[1],
        "w1": (n((K, H)) / np.sqrt(K) / s * u).astype(np.float32),
        "w2": (n((H, N)) / np.sqrt(H) / u[:, None]).astype(np.float32),
        "taps": (n((H, D)) / np.sqrt(D)).astype(np.float32),
        "offs": striped(np.random.permutation(T)[:S]),
    }


def reference(x_words, x_scales, w1, w2, taps, offs):
    xq = unpack_weight(x_words, x_scales)[:, unstriped(offs)]
    h = mxq(f64(w1), 0, "e4m3").T @ xq
    z = f64(taps)[:, 0:1] * h + f64(taps)[:, 1:2] * (np.pad(h, ((0, 0), (1, 0)))[:, :S])
    return mxq(f64(w2), 0, "e4m3").T @ mxq(z, 0, "e4m3")

@@ -1,0 +1,156 @@
+from contextlib import ExitStack
+
+import concourse.mybir as mybir
+
+K, T, S, H, N = 512, 2048, 1024, 512, 256
+FLOPS = 2 * K * H * S + 2 * H * N * S + 3 * H * S
+
+F32 = mybir.dt.float32
+BF16 = mybir.dt.bfloat16
+I32 = mybir.dt.int32
+U32 = mybir.dt.uint32
+U16 = mybir.dt.uint16
+U8 = mybir.dt.uint8
+FP8X4 = mybir.dt.float8_e4m3fn_x4
+MULT = mybir.AluOpType.mult
+ADD = mybir.AluOpType.add
+COPY = mybir.ActivationFunctionType.Copy
+
+P = 128
+PACK = 4
+W1_SPLIT = 80
+GATHER = 256
+PAD = 8
+CHUNKS = ((0, 256), (256, 256), (512, 256), (768, 128), (896, 128))
+SCALAR_BOTH_FROM = 896
+
+
+def tile_picked_dconv_none_p_kernel(tc, x_words, x_scales, w1, w2, taps, offs, out):
+    nc = tc.nc
+    with ExitStack() as ctx:
+        keep = ctx.enter_context(tc.tile_pool(name="keep", bufs=1))
+        ring = ctx.enter_context(tc.tile_pool(name="ring", bufs=3))
+        h_psum = ctx.enter_context(tc.psum_pool(name="h_psum", bufs=6))
+        o_psum = ctx.enter_context(tc.psum_pool(name="o_psum", bufs=2))
+
+        offsets = keep.tile([P, S // 16], U16, name="offsets")
+        x_scale_tab = keep.tile([P, T], U8, name="x_scale_tab", align_bytes=64)
+        x_word_tab = keep.tile([P, T], I32, name="x_word_tab", align_bytes=64)
+        tap = keep.tile([P, PACK, 2], F32, name="tap")
+        delayed = keep.tile([P, PACK, S + PAD], F32, name="delayed")
+
+        nc.vector.memset(x_scale_tab[:].bitcast(I32), 0)
+        nc.sync.dma_start(offsets[:], offs)
+        nc.sync.dma_start(tap[:], taps.rearrange("(p t) d -> p t d", t=PACK))
+        w1_rows = w1.rearrange("(p j) c -> p j c", j=PACK)
+        w1_raw = keep.tile([P, PACK, H], F32, name="w1_raw")
+        nc.sync.dma_start(w1_raw[:, 0:2, :], w1_rows[:, 0:2, :])
+        for q in range(4):
+            nc.sync.dma_start(x_scale_tab[32 * q : 32 * q + 4, :].bitcast(I32), x_scales[0, 4 * q : 4 * q + 4, :].bitcast(I32))
+        nc.sync.dma_start(w1_raw[:, 2:4, :], w1_rows[:, 2:4, :])
+        nc.sync.dma_start(x_word_tab[:], x_words[0].rearrange("p n r -> p (n r)").bitcast(I32))
+        w2_raw = keep.tile([P, PACK, N], F32, name="w2_raw")
+        nc.sync.dma_start(w2_raw[:], w2.rearrange("(p j) m -> p j m", j=PACK))
+        zero = keep.tile([P, PACK, 1], F32, name="zero")
+        nc.vector.memset(zero[:], 0.0)
+        nc.scalar.activation(delayed[:, :, 0:1], zero[:], COPY)
+
+        picked_scales = keep.tile([P, S], U8, name="picked_scales", align_bytes=64)
+        nc.vector.tensor_copy(picked_scales[:], x_scale_tab[:].indirect(offsets[:]))
+
+        w1_bf = keep.tile([P, PACK * H], BF16, name="w1_bf", align_bytes=64)
+        w1_dst = w1_bf[:].rearrange("p (t m j) -> p m j t", t=PACK, j=PACK)
+        w1_src = w1_raw[:].rearrange("p j (m t) -> p m j t", t=PACK)
+        nc.scalar.copy(w1_dst[:, :W1_SPLIT], w1_src[:, :W1_SPLIT])
+        nc.vector.tensor_copy(w1_dst[:, W1_SPLIT:], w1_src[:, W1_SPLIT:])
+        w1_codes = keep.tile([P, H], U32, name="w1_codes", align_bytes=64)
+        w1_scales = keep.tile([P, H], U8, name="w1_scales", align_bytes=64)
+        nc.vector.quantize_mx(out=w1_codes[:].bitcast(FP8X4), scales=w1_scales[:], in_=w1_bf[:])
+
+        picked_words = keep.tile([P, S], U32, name="picked_words", align_bytes=64)
+        for g0 in range(0, S, GATHER):
+            nc.vector.tensor_copy(
+                picked_words[:, g0 : g0 + GATHER],
+                x_word_tab[:].bitcast(U32).indirect(offsets[:, g0 // 16 : (g0 + GATHER) // 16]),
+            )
+
+        w2_bf = keep.tile([P, PACK * N], BF16, name="w2_bf", align_bytes=64)
+        w2_codes = keep.tile([P, N], U32, name="w2_codes", align_bytes=64)
+        w2_scales = keep.tile([P, N], U8, name="w2_scales", align_bytes=64)
+
+        out_rows = out.rearrange("(u p) s -> p u s", p=P)
+
+        def first_product(s0, n, per_bank):
+            h = []
+            for t0 in range(0, PACK, per_bank):
+                bank = h_psum.tile([P, per_bank, n], F32, name="h_bank")
+                for k in range(per_bank):
+                    t = t0 + k
+                    nc.tensor.matmul_mx(
+                        out=bank[:, k, :],
+                        lhsT=w1_codes[:, t * P : (t + 1) * P].bitcast(FP8X4),
+                        lhsT_scale=w1_scales[:, t * P : (t + 1) * P],
+                        rhs=picked_words[:, s0 : s0 + n].bitcast(FP8X4),
+                        rhs_scale=picked_scales[:, s0 : s0 + n],
+                        start=True,
+                        stop=True,
+                    )
+                    h.append(bank[:, k, :])
+            return h
+
+        def convolve(s0, n, per_bank, h):
+            z_bf = ring.tile([P, PACK * n], BF16, name="z_bf", align_bytes=64)
+            z_dst = z_bf[:].rearrange("p (c i t) -> p c t i", i=4, t=PACK)
+            if s0 >= SCALAR_BOTH_FROM:
+                current = ring.tile([P, PACK, n], F32, name="current")
+                for t in range(PACK):
+                    nc.scalar.activation(delayed[:, t, s0 + 1 : s0 + 1 + n], h[t], COPY, scale=tap[:, t, 1:2])
+                    nc.scalar.activation(current[:, t, :], h[t], COPY, scale=tap[:, t, 0:1])
+                nc.vector.tensor_tensor(
+                    z_dst,
+                    current[:].rearrange("p t (c i) -> p c t i", i=4),
+                    delayed[:, :, s0 : s0 + n].rearrange("p t (c i) -> p c t i", i=4),
+                    ADD,
+                )
+                return z_bf
+            planes = ring.tile([P, PACK, n], BF16, name="planes")
+            for t0 in range(0, PACK, per_bank):
+                for t in range(t0, t0 + per_bank):
+                    nc.scalar.activation(delayed[:, t, s0 + 1 : s0 + 1 + n], h[t], COPY, scale=tap[:, t, 1:2])
+                for t in range(t0, t0 + per_bank):
+                    nc.vector.scalar_tensor_tensor(planes[:, t, :], h[t], tap[:, t, 0:1], delayed[:, t, s0 : s0 + n], MULT, ADD)
+            nc.vector.tensor_copy(z_dst, planes[:].rearrange("p t (c i) -> p c t i", i=4))
+            return z_bf
+
+        def second_product(s0, n, z_bf):
+            z_codes = ring.tile([P, n], U32, name="z_codes", align_bytes=64)
+            z_scales = ring.tile([P, n], U8, name="z_scales", align_bytes=64)
+            nc.vector.quantize_mx(out=z_codes[:].bitcast(FP8X4), scales=z_scales[:], in_=z_bf[:])
+            acc = o_psum.tile([P, 2, n], F32, name="acc")
+            for u in range(2):
+                nc.tensor.matmul_mx(
+                    out=acc[:, u, :],
+                    lhsT=w2_codes[:, u * P : (u + 1) * P].bitcast(FP8X4),
+                    lhsT_scale=w2_scales[:, u * P : (u + 1) * P],
+                    rhs=z_codes[:].bitcast(FP8X4),
+                    rhs_scale=z_scales[:],
+                    start=True,
+                    stop=True,
+                )
+            result = ring.tile([P, 2, n], F32, name="result")
+            nc.scalar.copy(result[:], acc[:])
+            nc.sync.dma_start(out_rows[:, :, s0 : s0 + n], result[:])
+
+        pending = None
+        for c, (s0, n) in enumerate(CHUNKS):
+            per_bank = 1 if c == 0 else 2
+            z_bf = convolve(s0, n, per_bank, first_product(s0, n, per_bank))
+            if c == 1:
+                nc.scalar.copy(
+                    w2_bf[:].rearrange("p (c i j) -> p c j i", i=4, j=PACK), w2_raw[:].rearrange("p j (c i) -> p c j i", i=4)
+                )
+                nc.vector.quantize_mx(out=w2_codes[:].bitcast(FP8X4), scales=w2_scales[:], in_=w2_bf[:])
+            if pending is not None:
+                second_product(*pending)
+            pending = (s0, n, z_bf)
+        second_product(*pending)

@@ -18,139 +18,204 @@ COPY = mybir.ActivationFunctionType.Copy
 
 P = 128
 PACK = 4
-W1_SPLIT = 80
-GATHER = 256
-PAD = 8
-CHUNKS = ((0, 256), (256, 256), (512, 256), (768, 128), (896, 128))
-SCALAR_BOTH_FROM = 896
+HALF = 512
+W1_SPLIT = 64
+LAST = 128
 
 
 def tile_picked_dconv_none_p_kernel(tc, x_words, x_scales, w1, w2, taps, offs, out):
     nc = tc.nc
     with ExitStack() as ctx:
         keep = ctx.enter_context(tc.tile_pool(name="keep", bufs=1))
-        ring = ctx.enter_context(tc.tile_pool(name="ring", bufs=3))
-        h_psum = ctx.enter_context(tc.psum_pool(name="h_psum", bufs=6))
-        o_psum = ctx.enter_context(tc.psum_pool(name="o_psum", bufs=2))
+        psum = ctx.enter_context(tc.psum_pool(name="psum", bufs=8))
 
         offsets = keep.tile([P, S // 16], U16, name="offsets")
         x_scale_tab = keep.tile([P, T], U8, name="x_scale_tab", align_bytes=64)
         x_word_tab = keep.tile([P, T], I32, name="x_word_tab", align_bytes=64)
         tap = keep.tile([P, PACK, 2], F32, name="tap")
-        delayed = keep.tile([P, PACK, S + PAD], F32, name="delayed")
+        delayed = keep.tile([P, PACK, S + 8], F32, name="delayed")
+        zero = keep.tile([P, PACK, 1], F32, name="zero")
 
         nc.vector.memset(x_scale_tab[:].bitcast(I32), 0)
         nc.sync.dma_start(offsets[:], offs)
         nc.sync.dma_start(tap[:], taps.rearrange("(p t) d -> p t d", t=PACK))
         w1_rows = w1.rearrange("(p j) c -> p j c", j=PACK)
-        w1_raw = keep.tile([P, PACK, H], F32, name="w1_raw")
-        nc.sync.dma_start(w1_raw[:, 0:2, :], w1_rows[:, 0:2, :])
+        w1_raw = [keep.tile([P, PACK, H // 2], F32, name=f"w1_raw{u}", align_bytes=64) for u in range(2)]
+        nc.sync.dma_start(w1_raw[0][:], w1_rows[:, :, : H // 2])
         for q in range(4):
             nc.sync.dma_start(x_scale_tab[32 * q : 32 * q + 4, :].bitcast(I32), x_scales[0, 4 * q : 4 * q + 4, :].bitcast(I32))
-        nc.sync.dma_start(w1_raw[:, 2:4, :], w1_rows[:, 2:4, :])
         nc.sync.dma_start(x_word_tab[:], x_words[0].rearrange("p n r -> p (n r)").bitcast(I32))
+        nc.sync.dma_start(w1_raw[1][:], w1_rows[:, :, H // 2 :])
+        w1_src = [part[:].rearrange("p j (m t) -> p m j t", t=PACK) for part in w1_raw]
         w2_raw = keep.tile([P, PACK, N], F32, name="w2_raw")
         nc.sync.dma_start(w2_raw[:], w2.rearrange("(p j) m -> p j m", j=PACK))
-        zero = keep.tile([P, PACK, 1], F32, name="zero")
         nc.vector.memset(zero[:], 0.0)
         nc.scalar.activation(delayed[:, :, 0:1], zero[:], COPY)
 
         picked_scales = keep.tile([P, S], U8, name="picked_scales", align_bytes=64)
         nc.vector.tensor_copy(picked_scales[:], x_scale_tab[:].indirect(offsets[:]))
+        picked_words = {}
 
-        w1_bf = keep.tile([P, PACK * H], BF16, name="w1_bf", align_bytes=64)
-        w1_dst = w1_bf[:].rearrange("p (t m j) -> p m j t", t=PACK, j=PACK)
-        w1_src = w1_raw[:].rearrange("p j (m t) -> p m j t", t=PACK)
-        nc.scalar.copy(w1_dst[:, :W1_SPLIT], w1_src[:, :W1_SPLIT])
-        nc.vector.tensor_copy(w1_dst[:, W1_SPLIT:], w1_src[:, W1_SPLIT:])
+        def gather_words(s0, n, name):
+            words = keep.tile([P, n], U32, name=name, align_bytes=64)
+            nc.vector.tensor_copy(words[:], x_word_tab[:].bitcast(U32).indirect(offsets[:, s0 // 16 : (s0 + n) // 16]))
+            for c0 in range(0, n, 256):
+                picked_words[s0 + c0] = words[:, c0 : c0 + 256]
+
+        gather_words(0, 512, "words0")
+        gather_words(512, 256, "words1")
+
+        stage = keep.tile([P, PACK * S], BF16, name="stage", align_bytes=64)
+        w1_bf = stage[:, : PACK * H]
+        w1_dst = w1_bf.rearrange("p (t m j) -> p m j t", t=PACK, j=PACK)
+        nc.scalar.copy(w1_dst[:, :64], w1_src[0])
+        for t0 in (0, 2):
+            nc.scalar.copy(w1_dst[:, 64:, :, t0 : t0 + 2], w1_src[1][:, :, :, t0 : t0 + 2])
         w1_codes = keep.tile([P, H], U32, name="w1_codes", align_bytes=64)
         w1_scales = keep.tile([P, H], U8, name="w1_scales", align_bytes=64)
-        nc.vector.quantize_mx(out=w1_codes[:].bitcast(FP8X4), scales=w1_scales[:], in_=w1_bf[:])
+        for t in range(PACK):
+            cols = slice(t * P, (t + 1) * P)
+            nc.vector.quantize_mx(out=w1_codes[:, cols].bitcast(FP8X4), scales=w1_scales[:, cols], in_=w1_bf[:, t * H : (t + 1) * H])
 
-        picked_words = keep.tile([P, S], U32, name="picked_words", align_bytes=64)
-        for g0 in range(0, S, GATHER):
-            nc.vector.tensor_copy(
-                picked_words[:, g0 : g0 + GATHER],
-                x_word_tab[:].bitcast(U32).indirect(offsets[:, g0 // 16 : (g0 + GATHER) // 16]),
-            )
-
-        w2_bf = keep.tile([P, PACK * N], BF16, name="w2_bf", align_bytes=64)
+        gather_words(768, 256, "w1_raw1")
+        w2_bf = stage[:, 1024:2048]
         w2_codes = keep.tile([P, N], U32, name="w2_codes", align_bytes=64)
         w2_scales = keep.tile([P, N], U8, name="w2_scales", align_bytes=64)
-
+        planes = {}
+        current = keep.tile([P, PACK, LAST], F32, name="current")
+        z_codes = keep.tile([P, S], U32, name="z_codes", align_bytes=64)
+        z_scales = keep.tile([P, S], U8, name="z_scales", align_bytes=64)
         out_rows = out.rearrange("(u p) s -> p u s", p=P)
+        h = {}
+        for t in range(PACK):
+            h[0, t] = psum.tile([P, 256], F32, name="bank")[:]
+        for t0 in (0, 2):
+            pair = psum.tile([P, 2, 256], F32, name="bank")
+            h[256, t0], h[256, t0 + 1] = pair[:, 0, :], pair[:, 1, :]
+        for t in range(PACK):
+            h[512, t] = psum.tile([P, HALF], F32, name="bank")[:]
 
-        def first_product(s0, n, per_bank):
-            h = []
-            for t0 in range(0, PACK, per_bank):
-                bank = h_psum.tile([P, per_bank, n], F32, name="h_bank")
-                for k in range(per_bank):
-                    t = t0 + k
-                    nc.tensor.matmul_mx(
-                        out=bank[:, k, :],
-                        lhsT=w1_codes[:, t * P : (t + 1) * P].bitcast(FP8X4),
-                        lhsT_scale=w1_scales[:, t * P : (t + 1) * P],
-                        rhs=picked_words[:, s0 : s0 + n].bitcast(FP8X4),
-                        rhs_scale=picked_scales[:, s0 : s0 + n],
-                        start=True,
-                        stop=True,
-                    )
-                    h.append(bank[:, k, :])
-            return h
+        def h_cols(t, s0, n):
+            base = min(s0, HALF)
+            return h[base, t][:, s0 - base : s0 - base + n]
 
-        def convolve(s0, n, per_bank, h):
-            z_bf = ring.tile([P, PACK * n], BF16, name="z_bf", align_bytes=64)
-            z_dst = z_bf[:].rearrange("p (c i t) -> p c t i", i=4, t=PACK)
-            if s0 >= SCALAR_BOTH_FROM:
-                current = ring.tile([P, PACK, n], F32, name="current")
-                for t in range(PACK):
-                    nc.scalar.activation(delayed[:, t, s0 + 1 : s0 + 1 + n], h[t], COPY, scale=tap[:, t, 1:2])
-                    nc.scalar.activation(current[:, t, :], h[t], COPY, scale=tap[:, t, 0:1])
-                nc.vector.tensor_tensor(
-                    z_dst,
-                    current[:].rearrange("p t (c i) -> p c t i", i=4),
-                    delayed[:, :, s0 : s0 + n].rearrange("p t (c i) -> p c t i", i=4),
-                    ADD,
-                )
-                return z_bf
-            planes = ring.tile([P, PACK, n], BF16, name="planes")
-            for t0 in range(0, PACK, per_bank):
-                for t in range(t0, t0 + per_bank):
-                    nc.scalar.activation(delayed[:, t, s0 + 1 : s0 + 1 + n], h[t], COPY, scale=tap[:, t, 1:2])
-                for t in range(t0, t0 + per_bank):
-                    nc.vector.scalar_tensor_tensor(planes[:, t, :], h[t], tap[:, t, 0:1], delayed[:, t, s0 : s0 + n], MULT, ADD)
-            nc.vector.tensor_copy(z_dst, planes[:].rearrange("p t (c i) -> p c t i", i=4))
-            return z_bf
+        def by_fours(ap):
+            return ap.rearrange("p t (c i) -> p c t i", i=4)
 
-        def second_product(s0, n, z_bf):
-            z_codes = ring.tile([P, n], U32, name="z_codes", align_bytes=64)
-            z_scales = ring.tile([P, n], U8, name="z_scales", align_bytes=64)
-            nc.vector.quantize_mx(out=z_codes[:].bitcast(FP8X4), scales=z_scales[:], in_=z_bf[:])
-            acc = o_psum.tile([P, 2, n], F32, name="acc")
-            for u in range(2):
+        def place(s0):
+            return 256 - s0 if s0 < HALF else s0
+
+        def z_dst(s0, n):
+            return stage[:, PACK * place(s0) : PACK * (place(s0) + n)].rearrange("p (c i t) -> p c t i", i=4, t=PACK)
+
+        def first_product(s0, n, slots=range(PACK)):
+            for t in slots:
                 nc.tensor.matmul_mx(
-                    out=acc[:, u, :],
-                    lhsT=w2_codes[:, u * P : (u + 1) * P].bitcast(FP8X4),
-                    lhsT_scale=w2_scales[:, u * P : (u + 1) * P],
-                    rhs=z_codes[:].bitcast(FP8X4),
-                    rhs_scale=z_scales[:],
+                    out=h_cols(t, s0, n),
+                    lhsT=w1_codes[:, t * P : (t + 1) * P].bitcast(FP8X4),
+                    lhsT_scale=w1_scales[:, t * P : (t + 1) * P],
+                    rhs=picked_words[s0].bitcast(FP8X4),
+                    rhs_scale=picked_scales[:, s0 : s0 + n],
                     start=True,
                     stop=True,
                 )
-            result = ring.tile([P, 2, n], F32, name="result")
+
+        def delayed_tap(s0, n):
+            for t in range(PACK):
+                nc.scalar.activation(delayed[:, t, s0 + 1 : s0 + 1 + n], h_cols(t, s0, n), COPY, scale=tap[:, t, 1:2])
+
+        def combine(s0, n):
+            tile = keep.tile([P, PACK, n], BF16, name=f"planes{s0}")
+            for c0 in range(0, n, 128):
+                planes[s0 + c0] = (tile, c0)
+            for t in range(PACK):
+                nc.vector.scalar_tensor_tensor(
+                    tile[:, t, :], h_cols(t, s0, n), tap[:, t, 0:1], delayed[:, t, s0 : s0 + n], MULT, ADD
+                )
+
+        def interleave(s0, n):
+            tile, c0 = planes[s0]
+            nc.vector.tensor_copy(z_dst(s0, n), by_fours(tile[:, :, c0 : c0 + n]))
+
+        def interleave_g(s0, n):
+            tile, c0 = planes[s0]
+            nc.gpsimd.tensor_scalar(
+                stage[:, PACK * place(s0) : PACK * (place(s0) + n)].rearrange("p (c t) -> p c t", t=PACK),
+                tile[:, :, c0 : c0 + n].rearrange("p t c -> p c t"),
+                1.0,
+                0.0,
+                MULT,
+                ADD,
+            )
+
+        def quantize_z(s0, n):
+            nc.vector.quantize_mx(
+                out=z_codes[:, s0 : s0 + n].bitcast(FP8X4), scales=z_scales[:, s0 : s0 + n], in_=stage[:, PACK * s0 : PACK * (s0 + n)]
+            )
+
+        def second_matmul(acc, u, s0, n):
+            nc.tensor.matmul_mx(
+                out=acc,
+                lhsT=w2_codes[:, u * P : (u + 1) * P].bitcast(FP8X4),
+                lhsT_scale=w2_scales[:, u * P : (u + 1) * P],
+                rhs=z_codes[:, place(s0) : place(s0) + n].bitcast(FP8X4),
+                rhs_scale=z_scales[:, place(s0) : place(s0) + n],
+                start=True,
+                stop=True,
+            )
+
+        def second_product(s0, n):
+            acc = psum.tile([P, 2, n], F32, name="bank")
+            for u in range(2):
+                second_matmul(acc[:, u, :], u, s0, n)
+            result = keep.tile([P, 2, n], F32, name=f"result{s0}")
             nc.scalar.copy(result[:], acc[:])
             nc.sync.dma_start(out_rows[:, :, s0 : s0 + n], result[:])
 
-        pending = None
-        for c, (s0, n) in enumerate(CHUNKS):
-            per_bank = 1 if c == 0 else 2
-            z_bf = convolve(s0, n, per_bank, first_product(s0, n, per_bank))
-            if c == 1:
-                nc.scalar.copy(
-                    w2_bf[:].rearrange("p (c i j) -> p c j i", i=4, j=PACK), w2_raw[:].rearrange("p j (c i) -> p c j i", i=4)
-                )
-                nc.vector.quantize_mx(out=w2_codes[:].bitcast(FP8X4), scales=w2_scales[:], in_=w2_bf[:])
-            if pending is not None:
-                second_product(*pending)
-            pending = (s0, n, z_bf)
-        second_product(*pending)
+        def last_product(s0, n):
+            quantize_z(s0, n)
+            for u in range(2):
+                acc = psum.tile([P, n], F32, name="bank")
+                second_matmul(acc[:], u, s0, n)
+                result = keep.tile([P, n], F32, name=f"last{u}")
+                if u == 0:
+                    nc.scalar.copy(result[:], acc[:])
+                    nc.scalar.dma_start(out_rows[:, u, s0 : s0 + n], result[:])
+                else:
+                    nc.vector.tensor_copy(result[:], acc[:])
+                    nc.sync.dma_start(out_rows[:, u, s0 : s0 + n], result[:])
+
+        def both_taps(s0, n):
+            for t in range(PACK):
+                nc.scalar.activation(current[:, t, :], h_cols(t, s0, n), COPY, scale=tap[:, t, 0:1])
+            nc.vector.tensor_tensor(z_dst(s0, n), by_fours(current[:]), by_fours(delayed[:, :, s0 : s0 + n]), ADD)
+
+        w2_dst = w2_bf.rearrange("p (c j) -> p c j", j=PACK)
+        w2_src = w2_raw[:].rearrange("p j c -> p c j")
+
+        first_product(0, 256)
+        first_product(256, 256)
+        delayed_tap(0, 256)
+        nc.gpsimd.tensor_scalar(w2_dst, w2_src, 1.0, 0.0, MULT, ADD)
+        combine(0, 256)
+        nc.vector.quantize_mx(out=w2_codes[:].bitcast(FP8X4), scales=w2_scales[:], in_=w2_bf)
+        for t in range(PACK):
+            first_product(512, 256, (t,))
+            first_product(768, 256, (t,))
+        interleave_g(0, 256)
+        delayed_tap(256, 256)
+        combine(256, 256)
+        interleave_g(256, 256)
+        delayed_tap(512, 512)
+        combine(512, 384)
+        quantize_z(0, 512)
+        interleave(512, 256)
+        interleave(768, 128)
+        second_product(0, 256)
+        second_product(256, 256)
+        quantize_z(512, 256)
+        second_product(512, 256)
+        both_taps(896, 128)
+        quantize_z(768, 128)
+        second_product(768, 128)
+        last_product(896, 128)

@@ -38,14 +38,14 @@ def tile_picked_dconv_none_p_kernel(tc, x_words, x_scales, w1, w2, taps, offs, o
 
         nc.vector.memset(x_scale_tab[:].bitcast(I32), 0)
         nc.sync.dma_start(offsets[:], offs)
-        nc.sync.dma_start(tap[:], taps.rearrange("(p t) d -> p t d", t=PACK))
         w1_rows = w1.rearrange("(p j) c -> p j c", j=PACK)
         w1_raw = [keep.tile([P, PACK, H // 2], F32, name=f"w1_raw{u}", align_bytes=64) for u in range(2)]
         nc.sync.dma_start(w1_raw[0][:], w1_rows[:, :, : H // 2])
-        for q in range(4):
-            nc.sync.dma_start(x_scale_tab[32 * q : 32 * q + 4, :].bitcast(I32), x_scales[0, 4 * q : 4 * q + 4, :].bitcast(I32))
+        for r in range(4):
+            nc.sync.dma_start(x_scale_tab[r:P:32, :].bitcast(I32), x_scales[0, r:16:4, :].bitcast(I32))
         nc.sync.dma_start(x_word_tab[:], x_words[0].rearrange("p n r -> p (n r)").bitcast(I32))
         nc.sync.dma_start(w1_raw[1][:], w1_rows[:, :, H // 2 :])
+        nc.sync.dma_start(tap[:], taps.rearrange("(p t) d -> p t d", t=PACK))
         w1_src = [part[:].rearrange("p j (m t) -> p m j t", t=PACK) for part in w1_raw]
         w2_raw = keep.tile([P, PACK, N], F32, name="w2_raw")
         nc.sync.dma_start(w2_raw[:], w2.rearrange("(p j) m -> p j m", j=PACK))
@@ -103,7 +103,7 @@ def tile_picked_dconv_none_p_kernel(tc, x_words, x_scales, w1, w2, taps, offs, o
             return ap.rearrange("p t (c i) -> p c t i", i=4)
 
         def place(s0):
-            return 256 - s0 if s0 < HALF else s0
+            return max(s0, 256) if s0 < HALF else s0
 
         def z_dst(s0, n):
             return stage[:, PACK * place(s0) : PACK * (place(s0) + n)].rearrange("p (c i t) -> p c t i", i=4, t=PACK)
@@ -150,7 +150,7 @@ def tile_picked_dconv_none_p_kernel(tc, x_words, x_scales, w1, w2, taps, offs, o
 
         def quantize_z(s0, n):
             nc.vector.quantize_mx(
-                out=z_codes[:, s0 : s0 + n].bitcast(FP8X4), scales=z_scales[:, s0 : s0 + n], in_=stage[:, PACK * s0 : PACK * (s0 + n)]
+                out=z_codes[:, s0 : s0 + n].bitcast(FP8X4), scales=z_scales[:, s0 : s0 + n], in_=stage[:, PACK * place(s0) : PACK * (place(s0) + n)]
             )
 
         def second_matmul(acc, u, s0, n):
@@ -158,8 +158,8 @@ def tile_picked_dconv_none_p_kernel(tc, x_words, x_scales, w1, w2, taps, offs, o
                 out=acc,
                 lhsT=w2_codes[:, u * P : (u + 1) * P].bitcast(FP8X4),
                 lhsT_scale=w2_scales[:, u * P : (u + 1) * P],
-                rhs=z_codes[:, place(s0) : place(s0) + n].bitcast(FP8X4),
-                rhs_scale=z_scales[:, place(s0) : place(s0) + n],
+                rhs=z_codes[:, s0 : s0 + n].bitcast(FP8X4),
+                rhs_scale=z_scales[:, s0 : s0 + n],
                 start=True,
                 stop=True,
             )
@@ -205,17 +205,18 @@ def tile_picked_dconv_none_p_kernel(tc, x_words, x_scales, w1, w2, taps, offs, o
         interleave_g(0, 256)
         delayed_tap(256, 256)
         combine(256, 256)
+        quantize_z(0, 256)
         interleave_g(256, 256)
         delayed_tap(512, 512)
         combine(512, 384)
-        quantize_z(0, 512)
-        interleave(512, 256)
-        interleave(768, 128)
+        quantize_z(256, 256)
         second_product(0, 256)
         second_product(256, 256)
+        interleave(512, 256)
+        interleave(768, 128)
         quantize_z(512, 256)
-        second_product(512, 256)
         both_taps(896, 128)
+        second_product(512, 256)
         quantize_z(768, 128)
         second_product(768, 128)
         last_product(896, 128)

@@ -66,7 +66,7 @@ def tile_picked_dconv_none_p_kernel(tc, x_words, x_scales, w1, w2, taps, offs, o
         gather_words(512, 256, "words1")
 
         stage = keep.tile([P, PACK * S], BF16, name="stage", align_bytes=64)
-        w1_bf = stage[:, : PACK * H]
+        w1_bf = stage[:, PACK * H :]
         w1_dst = w1_bf.rearrange("p (t m j) -> p m j t", t=PACK, j=PACK)
         nc.scalar.copy(w1_dst[:, :64], w1_src[0])
         for t0 in (0, 2):
@@ -78,8 +78,7 @@ def tile_picked_dconv_none_p_kernel(tc, x_words, x_scales, w1, w2, taps, offs, o
             nc.vector.quantize_mx(out=w1_codes[:, cols].bitcast(FP8X4), scales=w1_scales[:, cols], in_=w1_bf[:, t * H : (t + 1) * H])
 
         gather_words(768, 256, "w1_raw1")
-        w2_bf = stage[:, 1024:2048]
-        w2_codes = keep.tile([P, N], U32, name="w2_codes", align_bytes=64)
+        w2_bf = stage[:, 3072:4096]
         w2_scales = keep.tile([P, N], U8, name="w2_scales", align_bytes=64)
         planes = {}
         current = keep.tile([P, PACK, LAST], F32, name="current")
@@ -103,7 +102,7 @@ def tile_picked_dconv_none_p_kernel(tc, x_words, x_scales, w1, w2, taps, offs, o
             return ap.rearrange("p t (c i) -> p c t i", i=4)
 
         def place(s0):
-            return max(s0, 256) if s0 < HALF else s0
+            return s0
 
         def z_dst(s0, n):
             return stage[:, PACK * place(s0) : PACK * (place(s0) + n)].rearrange("p (c i t) -> p c t i", i=4, t=PACK)
@@ -125,7 +124,7 @@ def tile_picked_dconv_none_p_kernel(tc, x_words, x_scales, w1, w2, taps, offs, o
                 nc.scalar.activation(delayed[:, t, s0 + 1 : s0 + 1 + n], h_cols(t, s0, n), COPY, scale=tap[:, t, 1:2])
 
         def combine(s0, n):
-            tile = keep.tile([P, PACK, n], BF16, name=f"planes{s0}")
+            tile = keep.tile([P, PACK, n], BF16, name=f"planes{s0}", align_bytes=64)
             for c0 in range(0, n, 128):
                 planes[s0 + c0] = (tile, c0)
             for t in range(PACK):
@@ -164,13 +163,21 @@ def tile_picked_dconv_none_p_kernel(tc, x_words, x_scales, w1, w2, taps, offs, o
                 stop=True,
             )
 
-        def second_product(s0, n):
+        def second_product(s0, n, copy):
             acc = psum.tile([P, 2, n], F32, name="bank")
             for u in range(2):
                 second_matmul(acc[:, u, :], u, s0, n)
             result = keep.tile([P, 2, n], F32, name=f"result{s0}")
-            nc.scalar.copy(result[:], acc[:])
+            copy(result[:], acc[:])
             nc.sync.dma_start(out_rows[:, :, s0 : s0 + n], result[:])
+
+        def wide_product(s0, n):
+            for u in range(2):
+                acc = psum.tile([P, n], F32, name="bank")
+                second_matmul(acc[:], u, s0, n)
+                result = keep.tile([P, n], F32, name=f"wide{u}")
+                nc.scalar.copy(result[:], acc[:])
+                nc.sync.dma_start(out_rows[:, u, s0 : s0 + n], result[:])
 
         def last_product(s0, n):
             quantize_z(s0, n)
@@ -198,25 +205,25 @@ def tile_picked_dconv_none_p_kernel(tc, x_words, x_scales, w1, w2, taps, offs, o
         delayed_tap(0, 256)
         nc.gpsimd.tensor_scalar(w2_dst, w2_src, 1.0, 0.0, MULT, ADD)
         combine(0, 256)
-        nc.vector.quantize_mx(out=w2_codes[:].bitcast(FP8X4), scales=w2_scales[:], in_=w2_bf)
         for t in range(PACK):
             first_product(512, 256, (t,))
             first_product(768, 256, (t,))
         interleave_g(0, 256)
         delayed_tap(256, 256)
         combine(256, 256)
-        quantize_z(0, 256)
         interleave_g(256, 256)
-        delayed_tap(512, 512)
+        delayed_tap(512, 384)
         combine(512, 384)
-        quantize_z(256, 256)
-        second_product(0, 256)
-        second_product(256, 256)
+        w2_codes = keep.tile([P, N], U32, name="planes256", align_bytes=64)
+        quantize_z(0, 512)
+        nc.vector.quantize_mx(out=w2_codes[:].bitcast(FP8X4), scales=w2_scales[:], in_=w2_bf)
         interleave(512, 256)
         interleave(768, 128)
+        delayed_tap(896, 128)
+        wide_product(0, 512)
         quantize_z(512, 256)
         both_taps(896, 128)
-        second_product(512, 256)
+        second_product(512, 256, nc.scalar.copy)
         quantize_z(768, 128)
-        second_product(768, 128)
+        second_product(768, 128, nc.vector.tensor_copy)
         last_product(896, 128)

@@ -19,7 +19,6 @@ COPY = mybir.ActivationFunctionType.Copy
 P = 128
 PACK = 4
 HALF = 512
-W1_SPLIT = 64
 LAST = 128
 
 
@@ -37,10 +36,10 @@ def tile_picked_dconv_none_p_kernel(tc, x_words, x_scales, w1, w2, taps, offs, o
         zero = keep.tile([P, PACK, 1], F32, name="zero")
 
         nc.vector.memset(x_scale_tab[:].bitcast(I32), 0)
-        nc.sync.dma_start(offsets[:], offs)
         w1_rows = w1.rearrange("(p j) c -> p j c", j=PACK)
         w1_raw = [keep.tile([P, PACK, H // 2], F32, name=f"w1_raw{u}", align_bytes=64) for u in range(2)]
         nc.sync.dma_start(w1_raw[0][:], w1_rows[:, :, : H // 2])
+        nc.sync.dma_start(offsets[:], offs)
         for r in range(4):
             nc.sync.dma_start(x_scale_tab[r:P:32, :].bitcast(I32), x_scales[0, r:16:4, :].bitcast(I32))
         nc.sync.dma_start(x_word_tab[:], x_words[0].rearrange("p n r -> p (n r)").bitcast(I32))
@@ -59,88 +58,99 @@ def tile_picked_dconv_none_p_kernel(tc, x_words, x_scales, w1, w2, taps, offs, o
         def gather_words(s0, n, name):
             words = keep.tile([P, n], U32, name=name, align_bytes=64)
             nc.vector.tensor_copy(words[:], x_word_tab[:].bitcast(U32).indirect(offsets[:, s0 // 16 : (s0 + n) // 16]))
-            for c0 in range(0, n, 256):
-                picked_words[s0 + c0] = words[:, c0 : c0 + 256]
+            for c0 in range(0, n, 64):
+                picked_words[s0 + c0] = (words, c0)
 
         gather_words(0, 512, "words0")
         gather_words(512, 256, "words1")
 
         stage = keep.tile([P, PACK * S], BF16, name="stage", align_bytes=64)
-        w1_bf = stage[:, PACK * H :]
-        w1_dst = w1_bf.rearrange("p (t m j) -> p m j t", t=PACK, j=PACK)
-        nc.scalar.copy(w1_dst[:, :64], w1_src[0])
-        for t0 in (0, 2):
-            nc.scalar.copy(w1_dst[:, 64:, :, t0 : t0 + 2], w1_src[1][:, :, :, t0 : t0 + 2])
+        w1_bf = [keep.tile([P, 2 * H], BF16, name=f"w1_bf{a}", align_bytes=64) for a in range(2)]
+        w1_dst = [part[:].rearrange("p (t m j) -> p m j t", t=2, j=PACK) for part in w1_bf]
+        for u in range(2):
+            for a in range(2):
+                nc.scalar.copy(w1_dst[a][:, 64 * u : 64 * (u + 1)], w1_src[u][:, :, :, 2 * a : 2 * a + 2])
         w1_codes = keep.tile([P, H], U32, name="w1_codes", align_bytes=64)
         w1_scales = keep.tile([P, H], U8, name="w1_scales", align_bytes=64)
-        for t in range(PACK):
-            cols = slice(t * P, (t + 1) * P)
-            nc.vector.quantize_mx(out=w1_codes[:, cols].bitcast(FP8X4), scales=w1_scales[:, cols], in_=w1_bf[:, t * H : (t + 1) * H])
 
-        gather_words(768, 256, "w1_raw1")
-        w2_bf = stage[:, 3072:4096]
+        def quantize_w1(t):
+            cols = slice(t * P, (t + 1) * P)
+            nc.vector.quantize_mx(
+                out=w1_codes[:, cols].bitcast(FP8X4), scales=w1_scales[:, cols], in_=w1_bf[t // 2][:, t % 2 * H : (t % 2 + 1) * H]
+            )
+
+        quantize_w1(0)
+        quantize_w1(1)
+        gather_words(768, 256, "w1_bf0")
+        quantize_w1(2)
+        quantize_w1(3)
+        w2_bf = keep.tile([P, PACK * N], BF16, name="w1_bf1", align_bytes=64)[:]
         w2_scales = keep.tile([P, N], U8, name="w2_scales", align_bytes=64)
         planes = {}
         current = keep.tile([P, PACK, LAST], F32, name="current")
         z_codes = keep.tile([P, S], U32, name="z_codes", align_bytes=64)
         z_scales = keep.tile([P, S], U8, name="z_scales", align_bytes=64)
+        z_words = {s0: z_codes[:, s0 : s0 + n] for s0, n in ((256, 256), (512, 256), (768, 128), (896, 128))}
         out_rows = out.rearrange("(u p) s -> p u s", p=P)
+        starts = (0, 256, 512, S - LAST)
         h = {}
+        for a, b in zip(starts, starts[1:]):
+            for t in range(PACK):
+                h[a, t] = psum.tile([P, b - a], F32, name="bank")[:]
+        last_bank = psum.tile([P, PACK, LAST], F32, name="bank")
         for t in range(PACK):
-            h[0, t] = psum.tile([P, 256], F32, name="bank")[:]
-        for t0 in (0, 2):
-            pair = psum.tile([P, 2, 256], F32, name="bank")
-            h[256, t0], h[256, t0 + 1] = pair[:, 0, :], pair[:, 1, :]
-        for t in range(PACK):
-            h[512, t] = psum.tile([P, HALF], F32, name="bank")[:]
+            h[S - LAST, t] = last_bank[:, t, :]
+
+        def chunk_of(s0):
+            return max(a for a in starts if a <= s0)
 
         def h_cols(t, s0, n):
-            base = min(s0, HALF)
+            base = chunk_of(s0)
             return h[base, t][:, s0 - base : s0 - base + n]
 
         def by_fours(ap):
             return ap.rearrange("p t (c i) -> p c t i", i=4)
 
-        def place(s0):
-            return s0
-
         def z_dst(s0, n):
-            return stage[:, PACK * place(s0) : PACK * (place(s0) + n)].rearrange("p (c i t) -> p c t i", i=4, t=PACK)
+            return stage[:, PACK * s0 : PACK * (s0 + n)].rearrange("p (c i t) -> p c t i", i=4, t=PACK)
 
-        def first_product(s0, n, slots=range(PACK)):
-            for t in slots:
-                nc.tensor.matmul_mx(
-                    out=h_cols(t, s0, n),
-                    lhsT=w1_codes[:, t * P : (t + 1) * P].bitcast(FP8X4),
-                    lhsT_scale=w1_scales[:, t * P : (t + 1) * P],
-                    rhs=picked_words[s0].bitcast(FP8X4),
-                    rhs_scale=picked_scales[:, s0 : s0 + n],
-                    start=True,
-                    stop=True,
-                )
+        def first_product(pieces):
+            for t in range(PACK):
+                for s0, n in pieces:
+                    words, c0 = picked_words[s0]
+                    nc.tensor.matmul_mx(
+                        out=h_cols(t, s0, n),
+                        lhsT=w1_codes[:, t * P : (t + 1) * P].bitcast(FP8X4),
+                        lhsT_scale=w1_scales[:, t * P : (t + 1) * P],
+                        rhs=words[:, c0 : c0 + n].bitcast(FP8X4),
+                        rhs_scale=picked_scales[:, s0 : s0 + n],
+                        start=True,
+                        stop=True,
+                    )
 
         def delayed_tap(s0, n):
             for t in range(PACK):
                 nc.scalar.activation(delayed[:, t, s0 + 1 : s0 + 1 + n], h_cols(t, s0, n), COPY, scale=tap[:, t, 1:2])
 
+        def current_tap(s0, n):
+            for t in range(PACK):
+                nc.scalar.activation(current[:, t, :], h_cols(t, s0, n), COPY, scale=tap[:, t, 0:1])
+
         def combine(s0, n):
-            tile = keep.tile([P, PACK, n], BF16, name=f"planes{s0}", align_bytes=64)
-            for c0 in range(0, n, 128):
-                planes[s0 + c0] = (tile, c0)
+            planes[s0] = keep.tile([P, PACK, n], BF16, name=f"planes{s0}", align_bytes=64)
             for t in range(PACK):
                 nc.vector.scalar_tensor_tensor(
-                    tile[:, t, :], h_cols(t, s0, n), tap[:, t, 0:1], delayed[:, t, s0 : s0 + n], MULT, ADD
+                    planes[s0][:, t, :], h_cols(t, s0, n), tap[:, t, 0:1], delayed[:, t, s0 : s0 + n], MULT, ADD
                 )
 
-        def interleave(s0, n):
-            tile, c0 = planes[s0]
-            nc.vector.tensor_copy(z_dst(s0, n), by_fours(tile[:, :, c0 : c0 + n]))
+        def interleave(s0, n, copy):
+            base = chunk_of(s0)
+            copy(z_dst(s0, n), by_fours(planes[base][:, :, s0 - base : s0 - base + n]))
 
         def interleave_g(s0, n):
-            tile, c0 = planes[s0]
             nc.gpsimd.tensor_scalar(
-                stage[:, PACK * place(s0) : PACK * (place(s0) + n)].rearrange("p (c t) -> p c t", t=PACK),
-                tile[:, :, c0 : c0 + n].rearrange("p t c -> p c t"),
+                stage[:, PACK * s0 : PACK * (s0 + n)].rearrange("p (c t) -> p c t", t=PACK),
+                planes[s0][:].rearrange("p t c -> p c t"),
                 1.0,
                 0.0,
                 MULT,
@@ -149,7 +159,7 @@ def tile_picked_dconv_none_p_kernel(tc, x_words, x_scales, w1, w2, taps, offs, o
 
         def quantize_z(s0, n):
             nc.vector.quantize_mx(
-                out=z_codes[:, s0 : s0 + n].bitcast(FP8X4), scales=z_scales[:, s0 : s0 + n], in_=stage[:, PACK * place(s0) : PACK * (place(s0) + n)]
+                out=z_words[s0].bitcast(FP8X4), scales=z_scales[:, s0 : s0 + n], in_=stage[:, PACK * s0 : PACK * (s0 + n)]
             )
 
         def second_matmul(acc, u, s0, n):
@@ -157,7 +167,7 @@ def tile_picked_dconv_none_p_kernel(tc, x_words, x_scales, w1, w2, taps, offs, o
                 out=acc,
                 lhsT=w2_codes[:, u * P : (u + 1) * P].bitcast(FP8X4),
                 lhsT_scale=w2_scales[:, u * P : (u + 1) * P],
-                rhs=z_codes[:, s0 : s0 + n].bitcast(FP8X4),
+                rhs=z_words[s0].bitcast(FP8X4),
                 rhs_scale=z_scales[:, s0 : s0 + n],
                 start=True,
                 stop=True,
@@ -171,16 +181,7 @@ def tile_picked_dconv_none_p_kernel(tc, x_words, x_scales, w1, w2, taps, offs, o
             copy(result[:], acc[:])
             nc.sync.dma_start(out_rows[:, :, s0 : s0 + n], result[:])
 
-        def wide_product(s0, n):
-            for u in range(2):
-                acc = psum.tile([P, n], F32, name="bank")
-                second_matmul(acc[:], u, s0, n)
-                result = keep.tile([P, n], F32, name=f"wide{u}")
-                nc.scalar.copy(result[:], acc[:])
-                nc.sync.dma_start(out_rows[:, u, s0 : s0 + n], result[:])
-
         def last_product(s0, n):
-            quantize_z(s0, n)
             for u in range(2):
                 acc = psum.tile([P, n], F32, name="bank")
                 second_matmul(acc[:], u, s0, n)
@@ -192,38 +193,37 @@ def tile_picked_dconv_none_p_kernel(tc, x_words, x_scales, w1, w2, taps, offs, o
                     nc.vector.tensor_copy(result[:], acc[:])
                     nc.sync.dma_start(out_rows[:, u, s0 : s0 + n], result[:])
 
-        def both_taps(s0, n):
-            for t in range(PACK):
-                nc.scalar.activation(current[:, t, :], h_cols(t, s0, n), COPY, scale=tap[:, t, 0:1])
-            nc.vector.tensor_tensor(z_dst(s0, n), by_fours(current[:]), by_fours(delayed[:, :, s0 : s0 + n]), ADD)
-
-        w2_dst = w2_bf.rearrange("p (c j) -> p c j", j=PACK)
-        w2_src = w2_raw[:].rearrange("p j c -> p c j")
-
-        first_product(0, 256)
-        first_product(256, 256)
+        first_product([[0,256]])
+        first_product([[256,256]])
         delayed_tap(0, 256)
-        nc.gpsimd.tensor_scalar(w2_dst, w2_src, 1.0, 0.0, MULT, ADD)
+        nc.gpsimd.tensor_scalar(
+            w2_bf.rearrange("p (c j) -> p c j", j=PACK), w2_raw[:].rearrange("p j c -> p c j"), 1.0, 0.0, MULT, ADD
+        )
         combine(0, 256)
-        for t in range(PACK):
-            first_product(512, 256, (t,))
-            first_product(768, 256, (t,))
+        first_product([[512,256],[768,128]])
         interleave_g(0, 256)
         delayed_tap(256, 256)
         combine(256, 256)
         interleave_g(256, 256)
+        first_product([[896, 128]])
         delayed_tap(512, 384)
         combine(512, 384)
-        w2_codes = keep.tile([P, N], U32, name="planes256", align_bytes=64)
-        quantize_z(0, 512)
-        nc.vector.quantize_mx(out=w2_codes[:].bitcast(FP8X4), scales=w2_scales[:], in_=w2_bf)
-        interleave(512, 256)
-        interleave(768, 128)
         delayed_tap(896, 128)
-        wide_product(0, 512)
+        current_tap(896, 128)
+        late_codes = keep.tile([P, N + 256], U32, name="planes256", align_bytes=64)
+        w2_codes = late_codes[:, :N]
+        z_words[0] = late_codes[:, N:]
+        nc.vector.quantize_mx(out=w2_codes.bitcast(FP8X4), scales=w2_scales[:], in_=w2_bf)
+        quantize_z(0, 256)
+        quantize_z(256, 256)
+        interleave(512, 256, nc.vector.tensor_copy)
+        second_product(0, 256, nc.scalar.copy)
+        interleave(768, 128, nc.vector.tensor_copy)
         quantize_z(512, 256)
-        both_taps(896, 128)
+        second_product(256, 256, nc.scalar.copy)
+        nc.vector.tensor_tensor(z_dst(896, 128), by_fours(current[:]), by_fours(delayed[:, :, 896 : 896 + 128]), ADD)
         second_product(512, 256, nc.scalar.copy)
         quantize_z(768, 128)
+        quantize_z(896, 128)
         second_product(768, 128, nc.vector.tensor_copy)
         last_product(896, 128)

@@ -42,8 +42,8 @@ def tile_picked_dconv_none_p_kernel(tc, x_words, x_scales, w1, w2, taps, offs, o
         nc.sync.dma_start(offsets[:], offs)
         for r in range(4):
             nc.sync.dma_start(x_scale_tab[r:P:32, :].bitcast(I32), x_scales[0, r:16:4, :].bitcast(I32))
-        nc.sync.dma_start(x_word_tab[:], x_words[0].rearrange("p n r -> p (n r)").bitcast(I32))
         nc.sync.dma_start(w1_raw[1][:], w1_rows[:, :, H // 2 :])
+        nc.sync.dma_start(x_word_tab[:], x_words[0].rearrange("p n r -> p (n r)").bitcast(I32))
         nc.sync.dma_start(tap[:], taps.rearrange("(p t) d -> p t d", t=PACK))
         w1_src = [part[:].rearrange("p j (m t) -> p m j t", t=PACK) for part in w1_raw]
         w2_raw = keep.tile([P, PACK, N], F32, name="w2_raw")
@@ -61,8 +61,6 @@ def tile_picked_dconv_none_p_kernel(tc, x_words, x_scales, w1, w2, taps, offs, o
             for c0 in range(0, n, 64):
                 picked_words[s0 + c0] = (words, c0)
 
-        gather_words(0, 512, "words0")
-        gather_words(512, 256, "words1")
 
         stage = keep.tile([P, PACK * S], BF16, name="stage", align_bytes=64)
         w1_bf = [keep.tile([P, 2 * H], BF16, name=f"w1_bf{a}", align_bytes=64) for a in range(2)]
@@ -81,25 +79,23 @@ def tile_picked_dconv_none_p_kernel(tc, x_words, x_scales, w1, w2, taps, offs, o
 
         quantize_w1(0)
         quantize_w1(1)
-        gather_words(768, 256, "w1_bf0")
         quantize_w1(2)
         quantize_w1(3)
-        w2_bf = keep.tile([P, PACK * N], BF16, name="w1_bf1", align_bytes=64)[:]
+        gather_words(0, 256, "words0")
+        gather_words(256, 256, "words1")
+        gather_words(512, 512, "words2")
+        w2_bf = keep.tile([P, PACK * N], BF16, name="x_word_tab", align_bytes=64)[:]
         w2_scales = keep.tile([P, N], U8, name="w2_scales", align_bytes=64)
         planes = {}
-        current = keep.tile([P, PACK, LAST], F32, name="current")
         z_codes = keep.tile([P, S], U32, name="z_codes", align_bytes=64)
         z_scales = keep.tile([P, S], U8, name="z_scales", align_bytes=64)
         z_words = {s0: z_codes[:, s0 : s0 + n] for s0, n in ((256, 256), (512, 256), (768, 128), (896, 128))}
         out_rows = out.rearrange("(u p) s -> p u s", p=P)
-        starts = (0, 256, 512, S - LAST)
+        starts = (0, 256, 512, 768, S)
         h = {}
         for a, b in zip(starts, starts[1:]):
             for t in range(PACK):
-                h[a, t] = psum.tile([P, b - a], F32, name="bank")[:]
-        last_bank = psum.tile([P, PACK, LAST], F32, name="bank")
-        for t in range(PACK):
-            h[S - LAST, t] = last_bank[:, t, :]
+                h[a, t] = psum.tile([P, b - a], F32, name="bank")
 
         def chunk_of(s0):
             return max(a for a in starts if a <= s0)
@@ -132,13 +128,10 @@ def tile_picked_dconv_none_p_kernel(tc, x_words, x_scales, w1, w2, taps, offs, o
             for t in range(PACK):
                 nc.scalar.activation(delayed[:, t, s0 + 1 : s0 + 1 + n], h_cols(t, s0, n), COPY, scale=tap[:, t, 1:2])
 
-        def current_tap(s0, n):
-            for t in range(PACK):
-                nc.scalar.activation(current[:, t, :], h_cols(t, s0, n), COPY, scale=tap[:, t, 0:1])
-
-        def combine(s0, n):
-            planes[s0] = keep.tile([P, PACK, n], BF16, name=f"planes{s0}", align_bytes=64)
-            for t in range(PACK):
+        def combine(s0, n, slots=range(PACK)):
+            if s0 not in planes:
+                planes[s0] = keep.tile([P, PACK, n], BF16, name=f"planes{s0}", align_bytes=64)
+            for t in slots:
                 nc.vector.scalar_tensor_tensor(
                     planes[s0][:, t, :], h_cols(t, s0, n), tap[:, t, 0:1], delayed[:, t, s0 : s0 + n], MULT, ADD
                 )
@@ -193,37 +186,38 @@ def tile_picked_dconv_none_p_kernel(tc, x_words, x_scales, w1, w2, taps, offs, o
                     nc.vector.tensor_copy(result[:], acc[:])
                     nc.sync.dma_start(out_rows[:, u, s0 : s0 + n], result[:])
 
-        first_product([[0,256]])
-        first_product([[256,256]])
+        first_product([[0, 256]])
+        first_product([[256, 256]])
         delayed_tap(0, 256)
         nc.gpsimd.tensor_scalar(
             w2_bf.rearrange("p (c j) -> p c j", j=PACK), w2_raw[:].rearrange("p j c -> p c j"), 1.0, 0.0, MULT, ADD
         )
         combine(0, 256)
-        first_product([[512,256],[768,128]])
+        first_product([[512, 256]])
         interleave_g(0, 256)
         delayed_tap(256, 256)
         combine(256, 256)
+        first_product([[768, 256]])
         interleave_g(256, 256)
-        first_product([[896, 128]])
-        delayed_tap(512, 384)
-        combine(512, 384)
-        delayed_tap(896, 128)
-        current_tap(896, 128)
+        delayed_tap(512, 256)
+        combine(512, 256)
+        delayed_tap(768, 256)
+        interleave(512, 256, nc.scalar.copy)
+        combine(768, 256, (0, 1))
         late_codes = keep.tile([P, N + 256], U32, name="planes256", align_bytes=64)
         w2_codes = late_codes[:, :N]
         z_words[0] = late_codes[:, N:]
         nc.vector.quantize_mx(out=w2_codes.bitcast(FP8X4), scales=w2_scales[:], in_=w2_bf)
         quantize_z(0, 256)
         quantize_z(256, 256)
-        interleave(512, 256, nc.vector.tensor_copy)
         second_product(0, 256, nc.scalar.copy)
-        interleave(768, 128, nc.vector.tensor_copy)
         quantize_z(512, 256)
         second_product(256, 256, nc.scalar.copy)
-        nc.vector.tensor_tensor(z_dst(896, 128), by_fours(current[:]), by_fours(delayed[:, :, 896 : 896 + 128]), ADD)
+        combine(768, 256, (2, 3))
         second_product(512, 256, nc.scalar.copy)
+        interleave(768, 128, nc.vector.tensor_copy)
+        interleave(896, 128, nc.vector.tensor_copy)
         quantize_z(768, 128)
         quantize_z(896, 128)
-        second_product(768, 128, nc.vector.tensor_copy)
+        second_product(768, 128, nc.scalar.copy)
         last_product(896, 128)

@@ -174,17 +174,13 @@ def tile_picked_dconv_none_p_kernel(tc, x_words, x_scales, w1, w2, taps, offs, o
             copy(result[:], acc[:])
             nc.sync.dma_start(out_rows[:, :, s0 : s0 + n], result[:])
 
-        def last_product(s0, n):
-            for u in range(2):
+        def shared_product(s0, n):
+            for u, copy in enumerate((nc.scalar.copy, nc.vector.tensor_copy)):
                 acc = psum.tile([P, n], F32, name="bank")
                 second_matmul(acc[:], u, s0, n)
-                result = keep.tile([P, n], F32, name=f"last{u}")
-                if u == 0:
-                    nc.scalar.copy(result[:], acc[:])
-                    nc.scalar.dma_start(out_rows[:, u, s0 : s0 + n], result[:])
-                else:
-                    nc.vector.tensor_copy(result[:], acc[:])
-                    nc.sync.dma_start(out_rows[:, u, s0 : s0 + n], result[:])
+                result = keep.tile([P, n], F32, name=f"shared{u}")
+                copy(result[:], acc[:])
+                nc.sync.dma_start(out_rows[:, u, s0 : s0 + n], result[:])
 
         first_product([[0, 256]])
         first_product([[256, 256]])
@@ -203,7 +199,7 @@ def tile_picked_dconv_none_p_kernel(tc, x_words, x_scales, w1, w2, taps, offs, o
         combine(512, 256)
         delayed_tap(768, 256)
         interleave(512, 256, nc.scalar.copy)
-        combine(768, 256, (0, 1))
+        combine(768, 256, (0, 1, 2))
         late_codes = keep.tile([P, N + 256], U32, name="planes256", align_bytes=64)
         w2_codes = late_codes[:, :N]
         z_words[0] = late_codes[:, N:]
@@ -211,13 +207,13 @@ def tile_picked_dconv_none_p_kernel(tc, x_words, x_scales, w1, w2, taps, offs, o
         quantize_z(0, 256)
         quantize_z(256, 256)
         second_product(0, 256, nc.scalar.copy)
+        combine(768, 256, (3,))
         quantize_z(512, 256)
         second_product(256, 256, nc.scalar.copy)
-        combine(768, 256, (2, 3))
-        second_product(512, 256, nc.scalar.copy)
         interleave(768, 128, nc.vector.tensor_copy)
         interleave(896, 128, nc.vector.tensor_copy)
         quantize_z(768, 128)
         quantize_z(896, 128)
+        shared_product(512, 256)
         second_product(768, 128, nc.scalar.copy)
-        last_product(896, 128)
+        second_product(896, 128, nc.vector.tensor_copy)

@@ -84,7 +84,7 @@ def tile_picked_dconv_none_p_kernel(tc, x_words, x_scales, w1, w2, taps, offs, o
         gather_words(0, 256, "words0")
         gather_words(256, 256, "words1")
         gather_words(512, 512, "words2")
-        w2_bf = keep.tile([P, PACK * N], BF16, name="x_word_tab", align_bytes=64)[:]
+        w2_bf = keep.tile([P, PACK * N], BF16, name="words0", align_bytes=64)[:]
         w2_scales = keep.tile([P, N], U8, name="w2_scales", align_bytes=64)
         planes = {}
         z_codes = keep.tile([P, S], U32, name="z_codes", align_bytes=64)

@@ -91,7 +91,7 @@ def tile_picked_dconv_none_p_kernel(tc, x_words, x_scales, w1, w2, taps, offs, o
         z_scales = keep.tile([P, S], U8, name="z_scales", align_bytes=64)
         z_words = {s0: z_codes[:, s0 : s0 + n] for s0, n in ((256, 256), (512, 256), (768, 128), (896, 128))}
         out_rows = out.rearrange("(u p) s -> p u s", p=P)
-        starts = (0, 256, 512, 768, S)
+        starts = (0, 256, 448, 768, S)
         h = {}
         for a, b in zip(starts, starts[1:]):
             for t in range(PACK):
@@ -183,20 +183,20 @@ def tile_picked_dconv_none_p_kernel(tc, x_words, x_scales, w1, w2, taps, offs, o
                 nc.sync.dma_start(out_rows[:, u, s0 : s0 + n], result[:])
 
         first_product([[0, 256]])
-        first_product([[256, 256]])
+        first_product([[256, 128], [384, 64]])
         delayed_tap(0, 256)
         nc.gpsimd.tensor_scalar(
             w2_bf.rearrange("p (c j) -> p c j", j=PACK), w2_raw[:].rearrange("p j c -> p c j"), 1.0, 0.0, MULT, ADD
         )
         combine(0, 256)
-        first_product([[512, 256]])
+        first_product([[448, 64], [512, 256]])
         interleave_g(0, 256)
-        delayed_tap(256, 256)
-        combine(256, 256)
+        delayed_tap(256, 192)
+        combine(256, 192)
         first_product([[768, 256]])
-        interleave_g(256, 256)
-        delayed_tap(512, 256)
-        combine(512, 256)
+        interleave_g(256, 192)
+        delayed_tap(448, 320)
+        combine(448, 320)
         delayed_tap(768, 256)
         interleave(512, 256, nc.scalar.copy)
         combine(768, 256, (0, 1, 2))
@@ -204,6 +204,7 @@ def tile_picked_dconv_none_p_kernel(tc, x_words, x_scales, w1, w2, taps, offs, o
         w2_codes = late_codes[:, :N]
         z_words[0] = late_codes[:, N:]
         nc.vector.quantize_mx(out=w2_codes.bitcast(FP8X4), scales=w2_scales[:], in_=w2_bf)
+        interleave(448, 64, nc.vector.tensor_copy)
         quantize_z(0, 256)
         quantize_z(256, 256)
         second_product(0, 256, nc.scalar.copy)

@@ -62,7 +62,16 @@ def tile_picked_dconv_none_p_kernel(tc, x_words, x_scales, w1, w2, taps, offs, o
                 picked_words[s0 + c0] = (words, c0)
 
 
-        stage = keep.tile([P, PACK * S], BF16, name="stage", align_bytes=64)
+        stage = {}
+
+        def new_stage(s0, n, tag):
+            tile = keep.tile([P, PACK * n], BF16, name=tag, align_bytes=64)
+            for c0 in range(0, n, 64):
+                stage[s0 + c0] = tile[:, PACK * c0 :]
+
+        def stage_cols(s0, n):
+            return stage[s0][:, : PACK * n]
+
         w1_bf = [keep.tile([P, 2 * H], BF16, name=f"w1_bf{a}", align_bytes=64) for a in range(2)]
         w1_dst = [part[:].rearrange("p (t m j) -> p m j t", t=2, j=PACK) for part in w1_bf]
         for u in range(2):
@@ -89,9 +98,9 @@ def tile_picked_dconv_none_p_kernel(tc, x_words, x_scales, w1, w2, taps, offs, o
         planes = {}
         z_codes = keep.tile([P, S], U32, name="z_codes", align_bytes=64)
         z_scales = keep.tile([P, S], U8, name="z_scales", align_bytes=64)
-        z_words = {s0: z_codes[:, s0 : s0 + n] for s0, n in ((256, 256), (512, 256), (768, 128), (896, 128))}
+        z_words = {s0: z_codes[:, s0 : s0 + n] for s0, n in ((512, 256), (768, 128), (896, 128))}
         out_rows = out.rearrange("(u p) s -> p u s", p=P)
-        starts = (0, 256, 448, 768, S)
+        starts = (0, 256, 512, 768, S)
         h = {}
         for a, b in zip(starts, starts[1:]):
             for t in range(PACK):
@@ -108,7 +117,7 @@ def tile_picked_dconv_none_p_kernel(tc, x_words, x_scales, w1, w2, taps, offs, o
             return ap.rearrange("p t (c i) -> p c t i", i=4)
 
         def z_dst(s0, n):
-            return stage[:, PACK * s0 : PACK * (s0 + n)].rearrange("p (c i t) -> p c t i", i=4, t=PACK)
+            return stage_cols(s0, n).rearrange("p (c i t) -> p c t i", i=4, t=PACK)
 
         def first_product(pieces):
             for t in range(PACK):
@@ -141,9 +150,10 @@ def tile_picked_dconv_none_p_kernel(tc, x_words, x_scales, w1, w2, taps, offs, o
             copy(z_dst(s0, n), by_fours(planes[base][:, :, s0 - base : s0 - base + n]))
 
         def interleave_g(s0, n):
+            base = chunk_of(s0)
             nc.gpsimd.tensor_scalar(
-                stage[:, PACK * s0 : PACK * (s0 + n)].rearrange("p (c t) -> p c t", t=PACK),
-                planes[s0][:].rearrange("p t c -> p c t"),
+                stage_cols(s0, n).rearrange("p (c t) -> p c t", t=PACK),
+                planes[base][:, :, s0 - base : s0 - base + n].rearrange("p t c -> p c t"),
                 1.0,
                 0.0,
                 MULT,
@@ -152,7 +162,7 @@ def tile_picked_dconv_none_p_kernel(tc, x_words, x_scales, w1, w2, taps, offs, o
 
         def quantize_z(s0, n):
             nc.vector.quantize_mx(
-                out=z_words[s0].bitcast(FP8X4), scales=z_scales[:, s0 : s0 + n], in_=stage[:, PACK * s0 : PACK * (s0 + n)]
+                out=z_words[s0].bitcast(FP8X4), scales=z_scales[:, s0 : s0 + n], in_=stage_cols(s0, n)
             )
 
         def second_matmul(acc, u, s0, n):
@@ -174,47 +184,45 @@ def tile_picked_dconv_none_p_kernel(tc, x_words, x_scales, w1, w2, taps, offs, o
             copy(result[:], acc[:])
             nc.sync.dma_start(out_rows[:, :, s0 : s0 + n], result[:])
 
-        def shared_product(s0, n):
-            for u, copy in enumerate((nc.scalar.copy, nc.vector.tensor_copy)):
-                acc = psum.tile([P, n], F32, name="bank")
-                second_matmul(acc[:], u, s0, n)
-                result = keep.tile([P, n], F32, name=f"shared{u}")
-                copy(result[:], acc[:])
-                nc.sync.dma_start(out_rows[:, u, s0 : s0 + n], result[:])
-
         first_product([[0, 256]])
-        first_product([[256, 128], [384, 64]])
+        first_product([[256, 256]])
         delayed_tap(0, 256)
         nc.gpsimd.tensor_scalar(
             w2_bf.rearrange("p (c j) -> p c j", j=PACK), w2_raw[:].rearrange("p j c -> p c j"), 1.0, 0.0, MULT, ADD
         )
         combine(0, 256)
-        first_product([[448, 64], [512, 256]])
+        first_product([[512, 256]])
+        new_stage(0, 256, "stage_a")
         interleave_g(0, 256)
-        delayed_tap(256, 192)
-        combine(256, 192)
+        delayed_tap(256, 256)
+        combine(256, 256)
         first_product([[768, 256]])
-        interleave_g(256, 192)
-        delayed_tap(448, 320)
-        combine(448, 320)
-        delayed_tap(768, 256)
-        interleave(512, 256, nc.scalar.copy)
-        combine(768, 256, (0, 1, 2))
-        late_codes = keep.tile([P, N + 256], U32, name="planes256", align_bytes=64)
-        w2_codes = late_codes[:, :N]
-        z_words[0] = late_codes[:, N:]
+        delayed_tap(512, 256)
+        new_stage(256, 320, "stage_b")
+        interleave(256, 256, nc.scalar.copy)
+        combine(512, 256, (0, 1))
+        early_codes = keep.tile([P, N + 256], U32, name="planes0", align_bytes=64)
+        w2_codes = early_codes[:, :N]
+        z_words[0] = early_codes[:, N:]
         nc.vector.quantize_mx(out=w2_codes.bitcast(FP8X4), scales=w2_scales[:], in_=w2_bf)
-        interleave(448, 64, nc.vector.tensor_copy)
         quantize_z(0, 256)
+        combine(512, 256, (2, 3))
+        delayed_tap(768, 256)
+        z_words[256] = keep.tile([P, 256], U32, name="codes256", align_bytes=64)[:]
+        for c0 in range(0, 256, 64):
+            stage[512 + c0] = stage[256][:, PACK * (64 + c0) :]
+        interleave(704, 64, nc.vector.tensor_copy)
         quantize_z(256, 256)
         second_product(0, 256, nc.scalar.copy)
-        combine(768, 256, (3,))
-        quantize_z(512, 256)
+        interleave_g(512, 192)
+        combine(768, 256)
         second_product(256, 256, nc.scalar.copy)
+        new_stage(768, 256, "stage_d")
         interleave(768, 128, nc.vector.tensor_copy)
+        quantize_z(512, 256)
         interleave(896, 128, nc.vector.tensor_copy)
         quantize_z(768, 128)
+        second_product(512, 256, nc.scalar.copy)
         quantize_z(896, 128)
-        shared_product(512, 256)
-        second_product(768, 128, nc.scalar.copy)
-        second_product(896, 128, nc.vector.tensor_copy)
+        second_product(768, 128, nc.vector.tensor_copy)
+        second_product(896, 128, nc.scalar.copy)

@@ -93,12 +93,16 @@ def tile_picked_dconv_none_p_kernel(tc, x_words, x_scales, w1, w2, taps, offs, o
         gather_words(0, 256, "words0")
         gather_words(256, 256, "words1")
         gather_words(512, 512, "words2")
-        w2_bf = keep.tile([P, PACK * N], BF16, name="words0", align_bytes=64)[:]
-        w2_scales = keep.tile([P, N], U8, name="w2_scales", align_bytes=64)
+        staged = keep.tile([P, PACK * (N + 576)], BF16, name="words0", align_bytes=64)
+        w2_bf = staged[:, : PACK * N]
+        for c0 in range(0, HALF, 64):
+            stage[c0] = staged[:, PACK * (N + c0) :]
         planes = {}
-        z_codes = keep.tile([P, S], U32, name="z_codes", align_bytes=64)
-        z_scales = keep.tile([P, S], U8, name="z_scales", align_bytes=64)
-        z_words = {s0: z_codes[:, s0 : s0 + n] for s0, n in ((512, 256), (768, 128), (896, 128))}
+        late_codes = keep.tile([P, N + S], U32, name="late_codes", align_bytes=64)
+        late_scales = keep.tile([P, N + S], U8, name="late_scales", align_bytes=64)
+        w2_codes, z_codes = late_codes[:, :N], late_codes[:, N:]
+        w2_scales, z_scales = late_scales[:, :N], late_scales[:, N:]
+        z_words = {s0: z_codes[:, s0 : s0 + n] for s0, n in ((0, 256), (256, 256), (512, 256), (768, 128), (896, 128))}
         out_rows = out.rearrange("(u p) s -> p u s", p=P)
         starts = (0, 256, 512, 768, S)
         h = {}
@@ -190,39 +194,42 @@ def tile_picked_dconv_none_p_kernel(tc, x_words, x_scales, w1, w2, taps, offs, o
         nc.gpsimd.tensor_scalar(
             w2_bf.rearrange("p (c j) -> p c j", j=PACK), w2_raw[:].rearrange("p j c -> p c j"), 1.0, 0.0, MULT, ADD
         )
+        early_planes = keep.tile([P, PACK, HALF], BF16, name="early_planes", align_bytes=64)
+        planes[0] = early_planes[:, :, :256]
+        planes[256] = early_planes[:, :, 256:]
         combine(0, 256)
         first_product([[512, 256]])
-        new_stage(0, 256, "stage_a")
-        interleave_g(0, 256)
+        interleave_g(0, 192)
         delayed_tap(256, 256)
         combine(256, 256)
         first_product([[768, 256]])
+        nc.gpsimd.tensor_scalar(
+            stage_cols(192, 128).rearrange("p (c t) -> p c t", t=PACK),
+            early_planes[:, :, 192:320].rearrange("p t c -> p c t"),
+            1.0,
+            0.0,
+            MULT,
+            ADD,
+        )
         delayed_tap(512, 256)
-        new_stage(256, 320, "stage_b")
-        interleave(256, 256, nc.scalar.copy)
-        combine(512, 256, (0, 1))
-        early_codes = keep.tile([P, N + 256], U32, name="planes0", align_bytes=64)
-        w2_codes = early_codes[:, :N]
-        z_words[0] = early_codes[:, N:]
-        nc.vector.quantize_mx(out=w2_codes.bitcast(FP8X4), scales=w2_scales[:], in_=w2_bf)
-        quantize_z(0, 256)
-        combine(512, 256, (2, 3))
+        interleave(320, 192, nc.scalar.copy)
+        combine(512, 256)
+        nc.vector.quantize_mx(out=late_codes[:, :HALF].bitcast(FP8X4), scales=late_scales[:, :HALF], in_=staged[:, : PACK * HALF])
         delayed_tap(768, 256)
-        z_words[256] = keep.tile([P, 256], U32, name="codes256", align_bytes=64)[:]
+        quantize_z(256, 256)
         for c0 in range(0, 256, 64):
             stage[512 + c0] = stage[256][:, PACK * (64 + c0) :]
         interleave(704, 64, nc.vector.tensor_copy)
-        quantize_z(256, 256)
         second_product(0, 256, nc.scalar.copy)
         interleave_g(512, 192)
         combine(768, 256)
         second_product(256, 256, nc.scalar.copy)
         new_stage(768, 256, "stage_d")
-        interleave(768, 128, nc.vector.tensor_copy)
         quantize_z(512, 256)
+        interleave(768, 128, nc.vector.tensor_copy)
         interleave(896, 128, nc.vector.tensor_copy)
-        quantize_z(768, 128)
         second_product(512, 256, nc.scalar.copy)
+        quantize_z(768, 128)
         quantize_z(896, 128)
-        second_product(768, 128, nc.vector.tensor_copy)
-        second_product(896, 128, nc.scalar.copy)
+        second_product(768, 128, nc.scalar.copy)
+        second_product(896, 128, nc.vector.tensor_copy)

@@ -18,8 +18,15 @@ COPY = mybir.ActivationFunctionType.Copy
 
 P = 128
 PACK = 4
-HALF = 512
-LAST = 128
+LIST_ROWS = 16
+QUADRANT = 32
+CHUNK = 256
+HALF = 2 * CHUNK
+LAST = CHUNK // 2
+
+FIRST_RUN_CUT = 240
+FIRST_RUN_END = 320
+SECOND_RUN = 192
 
 
 def tile_picked_dconv_none_p_kernel(tc, x_words, x_scales, w1, w2, taps, offs, out):
@@ -28,7 +35,7 @@ def tile_picked_dconv_none_p_kernel(tc, x_words, x_scales, w1, w2, taps, offs, o
         keep = ctx.enter_context(tc.tile_pool(name="keep", bufs=1))
         psum = ctx.enter_context(tc.psum_pool(name="psum", bufs=8))
 
-        offsets = keep.tile([P, S // 16], U16, name="offsets")
+        offsets = keep.tile([P, S // LIST_ROWS], U16, name="offsets")
         x_scale_tab = keep.tile([P, T], U8, name="x_scale_tab", align_bytes=64)
         x_word_tab = keep.tile([P, T], I32, name="x_word_tab", align_bytes=64)
         tap = keep.tile([P, PACK, 2], F32, name="tap")
@@ -37,136 +44,110 @@ def tile_picked_dconv_none_p_kernel(tc, x_words, x_scales, w1, w2, taps, offs, o
 
         nc.vector.memset(x_scale_tab[:].bitcast(I32), 0)
         w1_rows = w1.rearrange("(p j) c -> p j c", j=PACK)
-        w1_raw = [keep.tile([P, PACK, H // 2], F32, name=f"w1_raw{u}", align_bytes=64) for u in range(2)]
+        w1_raw = [keep.tile([P, PACK, H // 2], F32, name=f"w1_raw{half}", align_bytes=64) for half in range(2)]
         nc.sync.dma_start(w1_raw[0][:], w1_rows[:, :, : H // 2])
         nc.sync.dma_start(offsets[:], offs)
-        for r in range(4):
-            nc.sync.dma_start(x_scale_tab[r:P:32, :].bitcast(I32), x_scales[0, r:16:4, :].bitcast(I32))
+        for r in range(PACK):
+            nc.sync.dma_start(x_scale_tab[r:P:QUADRANT, :].bitcast(I32), x_scales[0, r : K // 32 : PACK, :].bitcast(I32))
         nc.sync.dma_start(w1_raw[1][:], w1_rows[:, :, H // 2 :])
         nc.sync.dma_start(x_word_tab[:], x_words[0].rearrange("p n r -> p (n r)").bitcast(I32))
         nc.sync.dma_start(tap[:], taps.rearrange("(p t) d -> p t d", t=PACK))
-        w1_src = [part[:].rearrange("p j (m t) -> p m j t", t=PACK) for part in w1_raw]
         w2_raw = keep.tile([P, PACK, N], F32, name="w2_raw")
         nc.sync.dma_start(w2_raw[:], w2.rearrange("(p j) m -> p j m", j=PACK))
+
         nc.vector.memset(zero[:], 0.0)
         nc.scalar.activation(delayed[:, :, 0:1], zero[:], COPY)
 
         picked_scales = keep.tile([P, S], U8, name="picked_scales", align_bytes=64)
         nc.vector.tensor_copy(picked_scales[:], x_scale_tab[:].indirect(offsets[:]))
-        picked_words = {}
 
-        def gather_words(s0, n, name):
-            words = keep.tile([P, n], U32, name=name, align_bytes=64)
-            nc.vector.tensor_copy(words[:], x_word_tab[:].bitcast(U32).indirect(offsets[:, s0 // 16 : (s0 + n) // 16]))
-            for c0 in range(0, n, 64):
-                picked_words[s0 + c0] = (words, c0)
-
-
-        stage = {}
-
-        def new_stage(s0, n, tag):
-            tile = keep.tile([P, PACK * n], BF16, name=tag, align_bytes=64)
-            for c0 in range(0, n, 64):
-                stage[s0 + c0] = tile[:, PACK * c0 :]
-
-        def stage_cols(s0, n):
-            return stage[s0][:, : PACK * n]
-
-        w1_bf = [keep.tile([P, 2 * H], BF16, name=f"w1_bf{a}", align_bytes=64) for a in range(2)]
-        w1_dst = [part[:].rearrange("p (t m j) -> p m j t", t=2, j=PACK) for part in w1_bf]
-        for u in range(2):
-            for a in range(2):
-                nc.scalar.copy(w1_dst[a][:, 64 * u : 64 * (u + 1)], w1_src[u][:, :, :, 2 * a : 2 * a + 2])
+        w1_src = [raw[:].rearrange("p j (m t) -> p m j t", t=PACK) for raw in w1_raw]
+        w1_bf = [keep.tile([P, 2 * H], BF16, name=f"w1_bf{pair}", align_bytes=64) for pair in range(2)]
+        w1_dst = [bf[:].rearrange("p (t m j) -> p m j t", t=2, j=PACK) for bf in w1_bf]
+        for half in range(2):
+            for pair in range(2):
+                nc.scalar.copy(
+                    w1_dst[pair][:, half * P // 2 : (half + 1) * P // 2], w1_src[half][:, :, :, 2 * pair : 2 * pair + 2]
+                )
         w1_codes = keep.tile([P, H], U32, name="w1_codes", align_bytes=64)
         w1_scales = keep.tile([P, H], U8, name="w1_scales", align_bytes=64)
-
-        def quantize_w1(t):
-            cols = slice(t * P, (t + 1) * P)
+        for t in range(PACK):
             nc.vector.quantize_mx(
-                out=w1_codes[:, cols].bitcast(FP8X4), scales=w1_scales[:, cols], in_=w1_bf[t // 2][:, t % 2 * H : (t % 2 + 1) * H]
+                out=w1_codes[:, t * P : (t + 1) * P].bitcast(FP8X4),
+                scales=w1_scales[:, t * P : (t + 1) * P],
+                in_=w1_bf[t // 2][:, t % 2 * H : (t % 2 + 1) * H],
             )
 
-        quantize_w1(0)
-        quantize_w1(1)
-        quantize_w1(2)
-        quantize_w1(3)
-        gather_words(0, 256, "words0")
-        gather_words(256, 256, "words1")
-        gather_words(512, 512, "words2")
-        staged = keep.tile([P, PACK * (N + 576)], BF16, name="words0", align_bytes=64)
+        picked_words = {}
+        for s0, n, name in ((0, CHUNK, "words0"), (CHUNK, CHUNK, "words1"), (HALF, HALF, "words2")):
+            words = keep.tile([P, n], U32, name=name, align_bytes=64)
+            entries = offsets[:, s0 // LIST_ROWS : (s0 + n) // LIST_ROWS]
+            nc.vector.tensor_copy(words[:], x_word_tab[:].bitcast(U32).indirect(entries))
+            for c0 in range(0, n, CHUNK):
+                picked_words[s0 + c0] = words[:, c0 : c0 + CHUNK]
+
+        vector_part = CHUNK - SECOND_RUN
+        staged = keep.tile([P, PACK * (N + HALF + vector_part)], BF16, name="words0", align_bytes=64)
         w2_bf = staged[:, : PACK * N]
-        for c0 in range(0, HALF, 64):
-            stage[c0] = staged[:, PACK * (N + c0) :]
+        stage = {0: staged[:, PACK * N :], HALF: staged[:, PACK * (N + CHUNK + vector_part) :]}
         planes = {}
         late_codes = keep.tile([P, N + S], U32, name="late_codes", align_bytes=64)
         late_scales = keep.tile([P, N + S], U8, name="late_scales", align_bytes=64)
         w2_codes, z_codes = late_codes[:, :N], late_codes[:, N:]
         w2_scales, z_scales = late_scales[:, :N], late_scales[:, N:]
-        z_words = {s0: z_codes[:, s0 : s0 + n] for s0, n in ((0, 256), (256, 256), (512, 256), (768, 128), (896, 128))}
         out_rows = out.rearrange("(u p) s -> p u s", p=P)
-        starts = (0, 256, 512, 768, S)
         h = {}
-        for a, b in zip(starts, starts[1:]):
+        for s0 in range(0, S, CHUNK):
             for t in range(PACK):
-                h[a, t] = psum.tile([P, b - a], F32, name="bank")
+                h[s0, t] = psum.tile([P, CHUNK], F32, name="bank")
 
-        def chunk_of(s0):
-            return max(a for a in starts if a <= s0)
+        def stage_cols(s0, n):
+            base = max(b for b in stage if b <= s0)
+            return stage[base][:, PACK * (s0 - base) : PACK * (s0 - base + n)]
 
-        def h_cols(t, s0, n):
-            base = chunk_of(s0)
-            return h[base, t][:, s0 - base : s0 - base + n]
+        def plane_cols(s0, n):
+            base = max(b for b in planes if b <= s0)
+            return planes[base][:, :, s0 - base : s0 - base + n]
 
-        def by_fours(ap):
-            return ap.rearrange("p t (c i) -> p c t i", i=4)
-
-        def z_dst(s0, n):
-            return stage_cols(s0, n).rearrange("p (c i t) -> p c t i", i=4, t=PACK)
-
-        def first_product(pieces):
+        def first_product(s0):
             for t in range(PACK):
-                for s0, n in pieces:
-                    words, c0 = picked_words[s0]
-                    nc.tensor.matmul_mx(
-                        out=h_cols(t, s0, n),
-                        lhsT=w1_codes[:, t * P : (t + 1) * P].bitcast(FP8X4),
-                        lhsT_scale=w1_scales[:, t * P : (t + 1) * P],
-                        rhs=words[:, c0 : c0 + n].bitcast(FP8X4),
-                        rhs_scale=picked_scales[:, s0 : s0 + n],
-                        start=True,
-                        stop=True,
-                    )
+                nc.tensor.matmul_mx(
+                    out=h[s0, t][:],
+                    lhsT=w1_codes[:, t * P : (t + 1) * P].bitcast(FP8X4),
+                    lhsT_scale=w1_scales[:, t * P : (t + 1) * P],
+                    rhs=picked_words[s0].bitcast(FP8X4),
+                    rhs_scale=picked_scales[:, s0 : s0 + CHUNK],
+                    start=True,
+                    stop=True,
+                )
 
-        def delayed_tap(s0, n):
+        def delayed_tap(s0):
             for t in range(PACK):
-                nc.scalar.activation(delayed[:, t, s0 + 1 : s0 + 1 + n], h_cols(t, s0, n), COPY, scale=tap[:, t, 1:2])
+                nc.scalar.activation(delayed[:, t, s0 + 1 : s0 + 1 + CHUNK], h[s0, t][:], COPY, scale=tap[:, t, 1:2])
 
-        def combine(s0, n, slots=range(PACK)):
-            if s0 not in planes:
-                planes[s0] = keep.tile([P, PACK, n], BF16, name=f"planes{s0}", align_bytes=64)
-            for t in slots:
+        def new_planes(s0, n):
+            planes[s0] = keep.tile([P, PACK, n], BF16, name=f"planes{s0}", align_bytes=64)
+
+        def combine(s0):
+            for t in range(PACK):
                 nc.vector.scalar_tensor_tensor(
-                    planes[s0][:, t, :], h_cols(t, s0, n), tap[:, t, 0:1], delayed[:, t, s0 : s0 + n], MULT, ADD
+                    plane_cols(s0, CHUNK)[:, t, :], h[s0, t][:], tap[:, t, 0:1], delayed[:, t, s0 : s0 + CHUNK], MULT, ADD
                 )
 
         def interleave(s0, n, copy):
-            base = chunk_of(s0)
-            copy(z_dst(s0, n), by_fours(planes[base][:, :, s0 - base : s0 - base + n]))
+            copy(
+                stage_cols(s0, n).rearrange("p (c i t) -> p c t i", i=4, t=PACK),
+                plane_cols(s0, n).rearrange("p t (c i) -> p c t i", i=4),
+            )
 
-        def interleave_g(s0, n):
-            base = chunk_of(s0)
+        def gpsimd_interleave(dst, src):
             nc.gpsimd.tensor_scalar(
-                stage_cols(s0, n).rearrange("p (c t) -> p c t", t=PACK),
-                planes[base][:, :, s0 - base : s0 - base + n].rearrange("p t c -> p c t"),
-                1.0,
-                0.0,
-                MULT,
-                ADD,
+                dst.rearrange("p (c t) -> p c t", t=PACK), src.rearrange("p t c -> p c t"), 1.0, 0.0, MULT, ADD
             )
 
         def quantize_z(s0, n):
             nc.vector.quantize_mx(
-                out=z_words[s0].bitcast(FP8X4), scales=z_scales[:, s0 : s0 + n], in_=stage_cols(s0, n)
+                out=z_codes[:, s0 : s0 + n].bitcast(FP8X4), scales=z_scales[:, s0 : s0 + n], in_=stage_cols(s0, n)
             )
 
         def second_matmul(acc, u, s0, n):
@@ -174,7 +155,7 @@ def tile_picked_dconv_none_p_kernel(tc, x_words, x_scales, w1, w2, taps, offs, o
                 out=acc,
                 lhsT=w2_codes[:, u * P : (u + 1) * P].bitcast(FP8X4),
                 lhsT_scale=w2_scales[:, u * P : (u + 1) * P],
-                rhs=z_words[s0].bitcast(FP8X4),
+                rhs=z_codes[:, s0 : s0 + n].bitcast(FP8X4),
                 rhs_scale=z_scales[:, s0 : s0 + n],
                 start=True,
                 stop=True,
@@ -188,48 +169,55 @@ def tile_picked_dconv_none_p_kernel(tc, x_words, x_scales, w1, w2, taps, offs, o
             copy(result[:], acc[:])
             nc.sync.dma_start(out_rows[:, :, s0 : s0 + n], result[:])
 
-        first_product([[0, 256]])
-        first_product([[256, 256]])
-        delayed_tap(0, 256)
-        nc.gpsimd.tensor_scalar(
-            w2_bf.rearrange("p (c j) -> p c j", j=PACK), w2_raw[:].rearrange("p j c -> p c j"), 1.0, 0.0, MULT, ADD
+        def second_product_by_blocks(s0, n):
+            for u in range(2):
+                acc = psum.tile([P, n], F32, name="bank")
+                second_matmul(acc[:], u, s0, n)
+                result = keep.tile([P, n], F32, name=f"block{u}")
+                nc.scalar.copy(result[:], acc[:])
+                nc.sync.dma_start(out_rows[:, u, s0 : s0 + n], result[:])
+
+        chunk0, chunk1, chunk2, chunk3 = range(0, S, CHUNK)
+
+        first_product(chunk0)
+        first_product(chunk1)
+        delayed_tap(chunk0)
+        gpsimd_interleave(w2_bf, w2_raw[:])
+        new_planes(chunk0, HALF)
+        combine(chunk0)
+        first_product(chunk2)
+        gpsimd_interleave(stage_cols(0, FIRST_RUN_CUT), plane_cols(0, FIRST_RUN_CUT))
+        delayed_tap(chunk1)
+        combine(chunk1)
+        first_product(chunk3)
+        second_piece = (FIRST_RUN_CUT, FIRST_RUN_END - FIRST_RUN_CUT)
+        gpsimd_interleave(stage_cols(*second_piece), plane_cols(*second_piece))
+        delayed_tap(chunk2)
+        interleave(FIRST_RUN_END, HALF - FIRST_RUN_END, nc.scalar.copy)
+        new_planes(chunk2, CHUNK)
+        combine(chunk2)
+
+        nc.vector.quantize_mx(
+            out=late_codes[:, : N + CHUNK].bitcast(FP8X4),
+            scales=late_scales[:, : N + CHUNK],
+            in_=staged[:, : PACK * (N + CHUNK)],
         )
-        early_planes = keep.tile([P, PACK, HALF], BF16, name="early_planes", align_bytes=64)
-        planes[0] = early_planes[:, :, :256]
-        planes[256] = early_planes[:, :, 256:]
-        combine(0, 256)
-        first_product([[512, 256]])
-        interleave_g(0, 192)
-        delayed_tap(256, 256)
-        combine(256, 256)
-        first_product([[768, 256]])
-        nc.gpsimd.tensor_scalar(
-            stage_cols(192, 128).rearrange("p (c t) -> p c t", t=PACK),
-            early_planes[:, :, 192:320].rearrange("p t c -> p c t"),
-            1.0,
-            0.0,
-            MULT,
-            ADD,
-        )
-        delayed_tap(512, 256)
-        interleave(320, 192, nc.scalar.copy)
-        combine(512, 256)
-        nc.vector.quantize_mx(out=late_codes[:, :HALF].bitcast(FP8X4), scales=late_scales[:, :HALF], in_=staged[:, : PACK * HALF])
-        delayed_tap(768, 256)
-        quantize_z(256, 256)
-        for c0 in range(0, 256, 64):
-            stage[512 + c0] = stage[256][:, PACK * (64 + c0) :]
-        interleave(704, 64, nc.vector.tensor_copy)
-        second_product(0, 256, nc.scalar.copy)
-        interleave_g(512, 192)
-        combine(768, 256)
-        second_product(256, 256, nc.scalar.copy)
-        new_stage(768, 256, "stage_d")
-        quantize_z(512, 256)
-        interleave(768, 128, nc.vector.tensor_copy)
-        interleave(896, 128, nc.vector.tensor_copy)
-        second_product(512, 256, nc.scalar.copy)
-        quantize_z(768, 128)
-        quantize_z(896, 128)
-        second_product(768, 128, nc.scalar.copy)
-        second_product(896, 128, nc.vector.tensor_copy)
+        delayed_tap(chunk3)
+        quantize_z(chunk1, CHUNK)
+        interleave(chunk2 + SECOND_RUN, vector_part, nc.vector.tensor_copy)
+        second_product(chunk0, CHUNK, nc.scalar.copy)
+
+        gpsimd_interleave(stage_cols(chunk2, SECOND_RUN), plane_cols(chunk2, SECOND_RUN))
+        new_planes(chunk3, CHUNK)
+        combine(chunk3)
+        second_product(chunk1, CHUNK, nc.scalar.copy)
+
+        stage[chunk3] = keep.tile([P, PACK * CHUNK], BF16, name="last_stage", align_bytes=64)[:]
+        quantize_z(chunk2, CHUNK)
+        interleave(chunk3, LAST, nc.vector.tensor_copy)
+        interleave(chunk3 + LAST, LAST, nc.vector.tensor_copy)
+        second_product_by_blocks(chunk2, CHUNK)
+        quantize_z(chunk3, LAST)
+        quantize_z(chunk3 + LAST, LAST)
+        second_product(chunk3, LAST, nc.scalar.copy)
+        second_product(chunk3 + LAST, LAST, nc.vector.tensor_copy)

@@ -26,7 +26,7 @@ LAST = CHUNK // 2
 
 FIRST_RUN_CUT = 240
 FIRST_RUN_END = 320
-SECOND_RUN = 192
+SECOND_RUN = 160
 
 
 def tile_picked_dconv_none_p_kernel(tc, x_words, x_scales, w1, w2, taps, offs, out):
@@ -204,7 +204,7 @@ def tile_picked_dconv_none_p_kernel(tc, x_words, x_scales, w1, w2, taps, offs, o
         )
         delayed_tap(chunk3)
         quantize_z(chunk1, CHUNK)
-        interleave(chunk2 + SECOND_RUN, vector_part, nc.vector.tensor_copy)
+        interleave(chunk2 + SECOND_RUN, vector_part, nc.scalar.copy)
         second_product(chunk0, CHUNK, nc.scalar.copy)
 
         gpsimd_interleave(stage_cols(chunk2, SECOND_RUN), plane_cols(chunk2, SECOND_RUN))

@@ -25,7 +25,7 @@ HALF = 2 * CHUNK
 LAST = CHUNK // 2
 
 FIRST_RUN_CUT = 240
-FIRST_RUN_END = 320
+FIRST_RUN_END = 288
 SECOND_RUN = 160
 
 
@@ -86,10 +86,10 @@ def tile_picked_dconv_none_p_kernel(tc, x_words, x_scales, w1, w2, taps, offs, o
             for c0 in range(0, n, CHUNK):
                 picked_words[s0 + c0] = words[:, c0 : c0 + CHUNK]
 
-        vector_part = CHUNK - SECOND_RUN
-        staged = keep.tile([P, PACK * (N + HALF + vector_part)], BF16, name="words0", align_bytes=64)
+        scalar_part = CHUNK - SECOND_RUN
+        staged = keep.tile([P, PACK * (N + HALF + scalar_part)], BF16, name="words0", align_bytes=64)
         w2_bf = staged[:, : PACK * N]
-        stage = {0: staged[:, PACK * N :], HALF: staged[:, PACK * (N + CHUNK + vector_part) :]}
+        stage = {0: staged[:, PACK * N :], HALF: staged[:, PACK * (N + CHUNK + scalar_part) :]}
         planes = {}
         late_codes = keep.tile([P, N + S], U32, name="late_codes", align_bytes=64)
         late_scales = keep.tile([P, N + S], U8, name="late_scales", align_bytes=64)
@@ -204,7 +204,7 @@ def tile_picked_dconv_none_p_kernel(tc, x_words, x_scales, w1, w2, taps, offs, o
         )
         delayed_tap(chunk3)
         quantize_z(chunk1, CHUNK)
-        interleave(chunk2 + SECOND_RUN, vector_part, nc.scalar.copy)
+        interleave(chunk2 + SECOND_RUN, scalar_part, nc.scalar.copy)
         second_product(chunk0, CHUNK, nc.scalar.copy)
 
         gpsimd_interleave(stage_cols(chunk2, SECOND_RUN), plane_cols(chunk2, SECOND_RUN))

@@ -44,12 +44,12 @@ def tile_picked_dconv_none_p_kernel(tc, x_words, x_scales, w1, w2, taps, offs, o
 
         nc.vector.memset(x_scale_tab[:].bitcast(I32), 0)
         w1_rows = w1.rearrange("(p j) c -> p j c", j=PACK)
-        w1_raw = [keep.tile([P, PACK, H // 2], F32, name=f"w1_raw{half}", align_bytes=64) for half in range(2)]
-        nc.sync.dma_start(w1_raw[0][:], w1_rows[:, :, : H // 2])
+        w1_raw = [keep.tile([P, 2, H], F32, name=f"w1_raw{half}", align_bytes=64) for half in range(2)]
+        nc.sync.dma_start(w1_raw[0][:], w1_rows[:, 0:2, :])
         nc.sync.dma_start(offsets[:], offs)
         for r in range(PACK):
             nc.sync.dma_start(x_scale_tab[r:P:QUADRANT, :].bitcast(I32), x_scales[0, r : K // 32 : PACK, :].bitcast(I32))
-        nc.sync.dma_start(w1_raw[1][:], w1_rows[:, :, H // 2 :])
+        nc.sync.dma_start(w1_raw[1][:], w1_rows[:, 2:4, :])
         nc.sync.dma_start(x_word_tab[:], x_words[0].rearrange("p n r -> p (n r)").bitcast(I32))
         nc.sync.dma_start(tap[:], taps.rearrange("(p t) d -> p t d", t=PACK))
         w2_raw = keep.tile([P, PACK, N], F32, name="w2_raw")
@@ -61,14 +61,12 @@ def tile_picked_dconv_none_p_kernel(tc, x_words, x_scales, w1, w2, taps, offs, o
         picked_scales = keep.tile([P, S], U8, name="picked_scales", align_bytes=64)
         nc.vector.tensor_copy(picked_scales[:], x_scale_tab[:].indirect(offsets[:]))
 
-        w1_src = [raw[:].rearrange("p j (m t) -> p m j t", t=PACK) for raw in w1_raw]
         w1_bf = [keep.tile([P, 2 * H], BF16, name=f"w1_bf{pair}", align_bytes=64) for pair in range(2)]
-        w1_dst = [bf[:].rearrange("p (t m j) -> p m j t", t=2, j=PACK) for bf in w1_bf]
         for half in range(2):
-            for pair in range(2):
-                nc.scalar.copy(
-                    w1_dst[pair][:, half * P // 2 : (half + 1) * P // 2], w1_src[half][:, :, :, 2 * pair : 2 * pair + 2]
-                )
+            src = w1_raw[half][:].rearrange("p j (m t) -> p m t j", t=PACK)
+            dst = [bf[:].rearrange("p (t m j) -> p m t j", t=2, j=PACK)[:, :, :, 2 * half : 2 * half + 2] for bf in w1_bf]
+            nc.scalar.copy(dst[0], src[:, :, 0:2, :])
+            nc.gpsimd.tensor_scalar(dst[1], src[:, :, 2:4, :], 1.0, 0.0, MULT, ADD)
         w1_codes = keep.tile([P, H], U32, name="w1_codes", align_bytes=64)
         w1_scales = keep.tile([P, H], U8, name="w1_scales", align_bytes=64)
         for t in range(PACK):

@@ -85,9 +85,9 @@ def tile_picked_dconv_none_p_kernel(tc, x_words, x_scales, w1, w2, taps, offs, o
                 picked_words[s0 + c0] = words[:, c0 : c0 + CHUNK]
 
         scalar_part = CHUNK - SECOND_RUN
-        staged = keep.tile([P, PACK * (N + HALF + scalar_part)], BF16, name="words0", align_bytes=64)
+        staged = keep.tile([P, PACK * (N + HALF)], BF16, name="words0", align_bytes=64)
         w2_bf = staged[:, : PACK * N]
-        stage = {0: staged[:, PACK * N :], HALF: staged[:, PACK * (N + CHUNK + scalar_part) :]}
+        stage = {0: staged[:, PACK * N :], HALF: w2_bf}
         planes = {}
         late_codes = keep.tile([P, N + S], U32, name="late_codes", align_bytes=64)
         late_scales = keep.tile([P, N + S], U8, name="late_scales", align_bytes=64)

@@ -26,7 +26,7 @@ LAST = CHUNK // 2
 
 FIRST_RUN_CUT = 240
 FIRST_RUN_END = 288
-SECOND_RUN = 160
+SECOND_RUN = 192
 
 
 def tile_picked_dconv_none_p_kernel(tc, x_words, x_scales, w1, w2, taps, offs, out):
@@ -87,7 +87,7 @@ def tile_picked_dconv_none_p_kernel(tc, x_words, x_scales, w1, w2, taps, offs, o
         scalar_part = CHUNK - SECOND_RUN
         staged = keep.tile([P, PACK * (N + HALF)], BF16, name="words0", align_bytes=64)
         w2_bf = staged[:, : PACK * N]
-        stage = {0: staged[:, PACK * N :], HALF: w2_bf}
+        stage = {0: staged[:, PACK * N :]}
         planes = {}
         late_codes = keep.tile([P, N + S], U32, name="late_codes", align_bytes=64)
         late_scales = keep.tile([P, N + S], U8, name="late_scales", align_bytes=64)
@@ -202,6 +202,7 @@ def tile_picked_dconv_none_p_kernel(tc, x_words, x_scales, w1, w2, taps, offs, o
         )
         delayed_tap(chunk3)
         quantize_z(chunk1, CHUNK)
+        stage[chunk2] = keep.tile([P, PACK * CHUNK], BF16, name="planes0", align_bytes=64)[:]
         interleave(chunk2 + SECOND_RUN, scalar_part, nc.scalar.copy)
         second_product(chunk0, CHUNK, nc.scalar.copy)
 

@@ -25,7 +25,7 @@ HALF = 2 * CHUNK
 LAST = CHUNK // 2
 
 FIRST_RUN_CUT = 240
-FIRST_RUN_END = 288
+FIRST_RUN_END = 272
 SECOND_RUN = 192
 
 

from contextlib import ExitStack

import concourse.mybir as mybir

K, T, S, H, N = 512, 2048, 1024, 512, 256
FLOPS = 2 * K * H * S + 2 * H * N * S + 3 * H * S

F32 = mybir.dt.float32
BF16 = mybir.dt.bfloat16
I32 = mybir.dt.int32
U32 = mybir.dt.uint32
U16 = mybir.dt.uint16
U8 = mybir.dt.uint8
FP8X4 = mybir.dt.float8_e4m3fn_x4
MULT = mybir.AluOpType.mult
ADD = mybir.AluOpType.add
COPY = mybir.ActivationFunctionType.Copy

P = 128
PACK = 4
LIST_ROWS = 16
QUADRANT = 32
CHUNK = 256
HALF = 2 * CHUNK
LAST = CHUNK // 2

FIRST_RUN_CUT = 240
FIRST_RUN_END = 272
SECOND_RUN = 192


def tile_picked_dconv_none_p_kernel(tc, x_words, x_scales, w1, w2, taps, offs, out):
    nc = tc.nc
    with ExitStack() as ctx:
        keep = ctx.enter_context(tc.tile_pool(name="keep", bufs=1))
        psum = ctx.enter_context(tc.psum_pool(name="psum", bufs=8))

        offsets = keep.tile([P, S // LIST_ROWS], U16, name="offsets")
        x_scale_tab = keep.tile([P, T], U8, name="x_scale_tab", align_bytes=64)
        x_word_tab = keep.tile([P, T], I32, name="x_word_tab", align_bytes=64)
        tap = keep.tile([P, PACK, 2], F32, name="tap")
        delayed = keep.tile([P, PACK, S + 8], F32, name="delayed")
        zero = keep.tile([P, PACK, 1], F32, name="zero")

        nc.vector.memset(x_scale_tab[:].bitcast(I32), 0)
        w1_rows = w1.rearrange("(p j) c -> p j c", j=PACK)
        w1_raw = [keep.tile([P, 2, H], F32, name=f"w1_raw{half}", align_bytes=64) for half in range(2)]
        nc.sync.dma_start(w1_raw[0][:], w1_rows[:, 0:2, :])
        nc.sync.dma_start(offsets[:], offs)
        for r in range(PACK):
            nc.sync.dma_start(x_scale_tab[r:P:QUADRANT, :].bitcast(I32), x_scales[0, r : K // 32 : PACK, :].bitcast(I32))
        nc.sync.dma_start(w1_raw[1][:], w1_rows[:, 2:4, :])
        nc.sync.dma_start(x_word_tab[:], x_words[0].rearrange("p n r -> p (n r)").bitcast(I32))
        nc.sync.dma_start(tap[:], taps.rearrange("(p t) d -> p t d", t=PACK))
        w2_raw = keep.tile([P, PACK, N], F32, name="w2_raw")
        nc.sync.dma_start(w2_raw[:], w2.rearrange("(p j) m -> p j m", j=PACK))

        nc.vector.memset(zero[:], 0.0)
        nc.scalar.activation(delayed[:, :, 0:1], zero[:], COPY)

        picked_scales = keep.tile([P, S], U8, name="picked_scales", align_bytes=64)
        nc.vector.tensor_copy(picked_scales[:], x_scale_tab[:].indirect(offsets[:]))

        w1_bf = [keep.tile([P, 2 * H], BF16, name=f"w1_bf{pair}", align_bytes=64) for pair in range(2)]
        for half in range(2):
            src = w1_raw[half][:].rearrange("p j (m t) -> p m t j", t=PACK)
            dst = [bf[:].rearrange("p (t m j) -> p m t j", t=2, j=PACK)[:, :, :, 2 * half : 2 * half + 2] for bf in w1_bf]
            nc.scalar.copy(dst[0], src[:, :, 0:2, :])
            nc.gpsimd.tensor_scalar(dst[1], src[:, :, 2:4, :], 1.0, 0.0, MULT, ADD)
        w1_codes = keep.tile([P, H], U32, name="w1_codes", align_bytes=64)
        w1_scales = keep.tile([P, H], U8, name="w1_scales", align_bytes=64)
        for t in range(PACK):
            nc.vector.quantize_mx(
                out=w1_codes[:, t * P : (t + 1) * P].bitcast(FP8X4),
                scales=w1_scales[:, t * P : (t + 1) * P],
                in_=w1_bf[t // 2][:, t % 2 * H : (t % 2 + 1) * H],
            )

        picked_words = {}
        for s0, n, name in ((0, CHUNK, "words0"), (CHUNK, CHUNK, "words1"), (HALF, HALF, "words2")):
            words = keep.tile([P, n], U32, name=name, align_bytes=64)
            entries = offsets[:, s0 // LIST_ROWS : (s0 + n) // LIST_ROWS]
            nc.vector.tensor_copy(words[:], x_word_tab[:].bitcast(U32).indirect(entries))
            for c0 in range(0, n, CHUNK):
                picked_words[s0 + c0] = words[:, c0 : c0 + CHUNK]

        scalar_part = CHUNK - SECOND_RUN
        staged = keep.tile([P, PACK * (N + HALF)], BF16, name="words0", align_bytes=64)
        w2_bf = staged[:, : PACK * N]
        stage = {0: staged[:, PACK * N :]}
        planes = {}
        late_codes = keep.tile([P, N + S], U32, name="late_codes", align_bytes=64)
        late_scales = keep.tile([P, N + S], U8, name="late_scales", align_bytes=64)
        w2_codes, z_codes = late_codes[:, :N], late_codes[:, N:]
        w2_scales, z_scales = late_scales[:, :N], late_scales[:, N:]
        out_rows = out.rearrange("(u p) s -> p u s", p=P)
        h = {}
        for s0 in range(0, S, CHUNK):
            for t in range(PACK):
                h[s0, t] = psum.tile([P, CHUNK], F32, name="bank")

        def stage_cols(s0, n):
            base = max(b for b in stage if b <= s0)
            return stage[base][:, PACK * (s0 - base) : PACK * (s0 - base + n)]

        def plane_cols(s0, n):
            base = max(b for b in planes if b <= s0)
            return planes[base][:, :, s0 - base : s0 - base + n]

        def first_product(s0):
            for t in range(PACK):
                nc.tensor.matmul_mx(
                    out=h[s0, t][:],
                    lhsT=w1_codes[:, t * P : (t + 1) * P].bitcast(FP8X4),
                    lhsT_scale=w1_scales[:, t * P : (t + 1) * P],
                    rhs=picked_words[s0].bitcast(FP8X4),
                    rhs_scale=picked_scales[:, s0 : s0 + CHUNK],
                    start=True,
                    stop=True,
                )

        def delayed_tap(s0):
            for t in range(PACK):
                nc.scalar.activation(delayed[:, t, s0 + 1 : s0 + 1 + CHUNK], h[s0, t][:], COPY, scale=tap[:, t, 1:2])

        def new_planes(s0, n):
            planes[s0] = keep.tile([P, PACK, n], BF16, name=f"planes{s0}", align_bytes=64)

        def combine(s0):
            for t in range(PACK):
                nc.vector.scalar_tensor_tensor(
                    plane_cols(s0, CHUNK)[:, t, :], h[s0, t][:], tap[:, t, 0:1], delayed[:, t, s0 : s0 + CHUNK], MULT, ADD
                )

        def interleave(s0, n, copy):
            copy(
                stage_cols(s0, n).rearrange("p (c i t) -> p c t i", i=4, t=PACK),
                plane_cols(s0, n).rearrange("p t (c i) -> p c t i", i=4),
            )

        def gpsimd_interleave(dst, src):
            nc.gpsimd.tensor_scalar(
                dst.rearrange("p (c t) -> p c t", t=PACK), src.rearrange("p t c -> p c t"), 1.0, 0.0, MULT, ADD
            )

        def quantize_z(s0, n):
            nc.vector.quantize_mx(
                out=z_codes[:, s0 : s0 + n].bitcast(FP8X4), scales=z_scales[:, s0 : s0 + n], in_=stage_cols(s0, n)
            )

        def second_matmul(acc, u, s0, n):
            nc.tensor.matmul_mx(
                out=acc,
                lhsT=w2_codes[:, u * P : (u + 1) * P].bitcast(FP8X4),
                lhsT_scale=w2_scales[:, u * P : (u + 1) * P],
                rhs=z_codes[:, s0 : s0 + n].bitcast(FP8X4),
                rhs_scale=z_scales[:, s0 : s0 + n],
                start=True,
                stop=True,
            )

        def second_product(s0, n, copy):
            acc = psum.tile([P, 2, n], F32, name="bank")
            for u in range(2):
                second_matmul(acc[:, u, :], u, s0, n)
            result = keep.tile([P, 2, n], F32, name=f"result{s0}")
            copy(result[:], acc[:])
            nc.sync.dma_start(out_rows[:, :, s0 : s0 + n], result[:])

        def second_product_by_blocks(s0, n):
            for u in range(2):
                acc = psum.tile([P, n], F32, name="bank")
                second_matmul(acc[:], u, s0, n)
                result = keep.tile([P, n], F32, name=f"block{u}")
                nc.scalar.copy(result[:], acc[:])
                nc.sync.dma_start(out_rows[:, u, s0 : s0 + n], result[:])

        chunk0, chunk1, chunk2, chunk3 = range(0, S, CHUNK)

        first_product(chunk0)
        first_product(chunk1)
        delayed_tap(chunk0)
        gpsimd_interleave(w2_bf, w2_raw[:])
        new_planes(chunk0, HALF)
        combine(chunk0)
        first_product(chunk2)
        gpsimd_interleave(stage_cols(0, FIRST_RUN_CUT), plane_cols(0, FIRST_RUN_CUT))
        delayed_tap(chunk1)
        combine(chunk1)
        first_product(chunk3)
        second_piece = (FIRST_RUN_CUT, FIRST_RUN_END - FIRST_RUN_CUT)
        gpsimd_interleave(stage_cols(*second_piece), plane_cols(*second_piece))
        delayed_tap(chunk2)
        interleave(FIRST_RUN_END, HALF - FIRST_RUN_END, nc.scalar.copy)
        new_planes(chunk2, CHUNK)
        combine(chunk2)

        nc.vector.quantize_mx(
            out=late_codes[:, : N + CHUNK].bitcast(FP8X4),
            scales=late_scales[:, : N + CHUNK],
            in_=staged[:, : PACK * (N + CHUNK)],
        )
        delayed_tap(chunk3)
        quantize_z(chunk1, CHUNK)
        stage[chunk2] = keep.tile([P, PACK * CHUNK], BF16, name="planes0", align_bytes=64)[:]
        interleave(chunk2 + SECOND_RUN, scalar_part, nc.scalar.copy)
        second_product(chunk0, CHUNK, nc.scalar.copy)

        gpsimd_interleave(stage_cols(chunk2, SECOND_RUN), plane_cols(chunk2, SECOND_RUN))
        new_planes(chunk3, CHUNK)
        combine(chunk3)
        second_product(chunk1, CHUNK, nc.scalar.copy)

        stage[chunk3] = keep.tile([P, PACK * CHUNK], BF16, name="last_stage", align_bytes=64)[:]
        quantize_z(chunk2, CHUNK)
        interleave(chunk3, LAST, nc.vector.tensor_copy)
        interleave(chunk3 + LAST, LAST, nc.vector.tensor_copy)
        second_product_by_blocks(chunk2, CHUNK)
        quantize_z(chunk3, LAST)
        quantize_z(chunk3 + LAST, LAST)
        second_product(chunk3, LAST, nc.scalar.copy)
        second_product(chunk3 + LAST, LAST, nc.vector.tensor_copy)
